import numpy as np
import ml_dtypes


def mxq(x, axis, fmt="e4m3"):
    dtype, down = {"e4m3": (ml_dtypes.float8_e4m3fn, 7), "e5m2": (ml_dtypes.float8_e5m2, 14)}[fmt]
    v = np.moveaxis(np.asarray(x, np.float32).astype(ml_dtypes.bfloat16).astype(np.float64), axis, -1)
    blocks = v.reshape(v.shape[:-1] + (-1, 32))
    amax = np.abs(blocks).max(-1, keepdims=True)
    byte = np.maximum(np.where(amax > 0, np.frexp(amax)[1] - 1 + 127, 0) - down, 1)
    scale = np.exp2(byte - 127.0)
    codes = (blocks / scale).astype(np.float32).astype(dtype).astype(np.float64)
    return np.moveaxis((codes * scale).reshape(v.shape), -1, axis)


WIDE = False


def mx_kscale(k):
    if not WIDE:
        return np.ones(k)
    levels = np.array([10, -10, 5, -5, 0])
    if k % 512:
        return np.exp2(np.random.permutation(np.resize(levels, k // 32))).repeat(32)
    a = np.empty((k // 512, 16))
    for p in range(k // 512):
        a[p, :8] = np.random.permutation(np.resize(levels, 8))
        for g in range(8):
            far = levels[np.abs(levels - a[p, g]) >= 10]
            a[p, g + 8] = far[np.random.randint(len(far))]
    return np.exp2(a.ravel()).repeat(32)


def f64(x):
    return np.asarray(x).astype(np.float64)


def striped(idx):
    return np.tile(np.asarray(idx).reshape(-1, 16).T, (8, 1)).astype(np.uint16)


def unstriped(offs):
    return offs[:16].T.reshape(-1).astype(np.int64)


E2M1 = np.array([0.0, 0.5, 1.0, 1.5, 2.0, 3.0, 4.0, 6.0, -0.0, -0.5, -1.0, -1.5, -2.0, -3.0, -4.0, -6.0])


def pack_weight(w, fmt):
    k, n = w.shape
    w = f64(np.asarray(w, np.float32).astype(ml_dtypes.bfloat16)).reshape(k // 32, 32, n)
    amax = np.abs(w).max(1)
    if fmt == "e4m3":
        byte = np.frexp(amax)[1] - 1 + 127 - 7
    else:
        mant, ex = np.frexp(amax / 6.0)
        byte = np.where(mant > 0.5, ex, ex - 1) + 127
    byte = np.clip(np.where(amax > 0, byte, 1), 1, 254)
    scaled = (w * np.exp2(127.0 - byte)[:, None, :]).reshape(k, n).astype(np.float32)
    by_word = np.ascontiguousarray(scaled.reshape(k // 512, 128, 4, n).transpose(0, 1, 3, 2))
    if fmt == "e4m3":
        words = by_word.astype(ml_dtypes.float8_e4m3fn).view(np.uint8)
    else:
        c = by_word.astype(ml_dtypes.float4_e2m1fn).view(np.uint8) & 0xF
        words = (c[..., 0::2] | (c[..., 1::2] << 4)).reshape(k // 512, 128, 2 * n)
    return np.ascontiguousarray(words), np.ascontiguousarray(byte.astype(np.uint8).reshape(k // 512, 16, n))


def unpack_weight(words, scales, fmt):
    g, _, n = scales.shape
    words = np.ascontiguousarray(words).reshape(g, 128, n, -1)
    if fmt == "e4m3":
        vals = words.view(ml_dtypes.float8_e4m3fn).astype(np.float64)
    else:
        nib = np.empty((g, 128, n, 4), np.uint8)
        nib[..., 0::2] = words & 0xF
        nib[..., 1::2] = words >> 4
        vals = E2M1[nib]
    vals = vals * np.repeat(np.exp2(scales.astype(np.float64) - 127.0), 8, axis=1)[..., None]
    return vals.transpose(0, 1, 3, 2).reshape(g * 512, n)


D, T, I, Q = 512, 2048, 512, 128


def setup_inputs():
    n = np.random.standard_normal
    idx = np.random.permutation(T)[:I]
    fd = mx_kscale(D)
    keysp = pack_weight(n((D, T)) / fd[:, None], "e4m3")
    return {
        "query": (n((D, Q)) * 0.8 / np.sqrt(D) * fd[:, None]).astype(np.float32),
        "keys_words": keysp[0],
        "keys_scales": keysp[1],
        "mass": (np.random.uniform(0.0, 2.0, (Q, T))).astype(np.float32),
        "dec": (np.random.uniform(0.8, 1.0, (Q, 1))).astype(np.float32),
        "offs": striped(idx),
    }


def reference(query, keys_words, keys_scales, mass, dec, offs):
    idx = unstriped(offs)
    keysu = unpack_weight(keys_words, keys_scales, "e4m3")
    queryq = mxq(f64(query), 0, "e4m3")
    keysidxg = keysu[:, idx]
    a = queryq.T @ keysidxg
    p = np.exp(a - np.max(a, axis=1, keepdims=True))
    w = p / np.sum(p, axis=1, keepdims=True) * 512.0
    wf = np.zeros((Q, T))
    wf[:, idx] = w
    y = f64(dec) * f64(mass) + wf
    return y

@@ -1,0 +1,106 @@
+from contextlib import ExitStack
+
+import concourse.mybir as mybir
+
+D, T, SLOTS, Q = 512, 2048, 512, 128
+FLOPS = 2 * D * SLOTS * Q
+
+F32 = mybir.dt.float32
+BF16 = mybir.dt.bfloat16
+I32 = mybir.dt.int32
+U32 = mybir.dt.uint32
+U16 = mybir.dt.uint16
+U8 = mybir.dt.uint8
+FP8X4 = mybir.dt.float8_e4m3fn_x4
+ALU = mybir.AluOpType
+ACT = mybir.ActivationFunctionType
+
+P = 128
+HALF = SLOTS // 2
+OUT_WIDTHS = (256, 512, 512, 512, 256)
+
+
+def tile_attend_heavyhitter_kernel(tc, query, keys_words, keys_scales, mass, dec, offs, out):
+    nc = tc.nc
+    with ExitStack() as ctx:
+        sb = ctx.enter_context(tc.tile_pool(name="sb", bufs=1))
+        ps = ctx.enter_context(tc.psum_pool(name="ps", bufs=1))
+
+        offsets = sb.tile([P, SLOTS // 16], U16, name="offsets")
+        q_raw = sb.tile([P, 4, Q], F32, name="q_raw", tag="raw")
+        pool_scales = sb.tile([P, T], U8, name="pool_scales", align_bytes=64)
+        pool_words = sb.tile([P, T], I32, name="pool_words", align_bytes=64)
+        dec_sb = sb.tile([P, 1], F32, name="dec_sb")
+        placed = sb.tile([P, T], F32, name="placed")
+
+        nc.vector.memset(pool_scales[:].bitcast(I32), 0)
+        nc.sync.dma_start(offsets[:], offs)
+        nc.sync.dma_start(dec_sb[:], dec)
+        nc.sync.dma_start(q_raw[:], query.rearrange("(p j) q -> p j q", j=4))
+        for quad in range(4):
+            nc.sync.dma_start(
+                pool_scales[32 * quad : 32 * quad + 4, :].bitcast(I32),
+                keys_scales[0, 4 * quad : 4 * quad + 4, :].bitcast(I32),
+            )
+        nc.sync.dma_start(pool_words[:], keys_words[0].rearrange("p n t -> p (n t)").bitcast(I32))
+        nc.vector.memset(placed[:], 0.0)
+
+        q_bf = sb.tile([P, Q, 4], BF16, name="q_bf", align_bytes=64)
+        nc.scalar.copy(q_bf[:], q_raw[:].rearrange("p j q -> p q j"))
+        mass_sb = sb.tile([P, T], F32, name="mass_sb", tag="raw")
+        nc.sync.dma_start(mass_sb[:], mass)
+        q_codes = sb.tile([P, Q], U32, name="q_codes", align_bytes=64)
+        q_scales = sb.tile([P, Q], U8, name="q_scales", align_bytes=64)
+        nc.vector.quantize_mx(
+            out=q_codes[:].bitcast(FP8X4), scales=q_scales[:], in_=q_bf[:].rearrange("p q j -> p (q j)")
+        )
+
+        k_scales = sb.tile([P, SLOTS], U8, name="k_scales", align_bytes=64)
+        nc.vector.tensor_copy(k_scales[:], pool_scales[:].indirect(offsets[:]))
+
+        halves = [slice(h * HALF, (h + 1) * HALF) for h in range(2)]
+        half_offsets = [offsets[:, h * HALF // 16 : (h + 1) * HALF // 16] for h in range(2)]
+        k_words = [sb.tile([P, HALF], U32, name="k_words%d" % h, align_bytes=64) for h in range(2)]
+        scores = [ps.tile([P, HALF], F32, name="scores%d" % h) for h in range(2)]
+        for h in range(2):
+            nc.vector.tensor_copy(k_words[h][:], pool_words[:].bitcast(U32).indirect(half_offsets[h]))
+            nc.tensor.matmul_mx(
+                out=scores[h][:],
+                lhsT=q_codes[:].bitcast(FP8X4),
+                lhsT_scale=q_scales[:],
+                rhs=k_words[h][:].bitcast(FP8X4),
+                rhs_scale=k_scales[:, halves[h]],
+                start=True,
+                stop=True,
+            )
+
+        neg_max_first = sb.tile([P, 1], F32, name="neg_max_first")
+        neg_max = sb.tile([P, 1], F32, name="neg_max")
+        nc.vector.tensor_reduce(neg_max_first[:], scores[0][:], mybir.AxisListType.X, ALU.max, negate=True)
+        neg_second = sb.tile([P, HALF], F32, name="neg_second", tag="reused")
+        nc.vector.tensor_scalar(
+            neg_second[:], scores[1][:], -1.0, neg_max_first[:], ALU.mult, ALU.min, accum_out=neg_max[:]
+        )
+
+        sums = sb.tile([P, 2], F32, name="sums")
+        probs = [sb.tile([P, HALF], F32, name="probs%d" % h) for h in range(2)]
+        nc.scalar.activation(probs[0][:], scores[0][:], ACT.Exp, bias=neg_max[:], scale=1.0, accum_out=sums[:, 0:1])
+        nc.scalar.activation(probs[1][:], neg_second[:], ACT.Exp, bias=neg_max[:], scale=-1.0, accum_out=sums[:, 1:2])
+        sums_scaled = sb.tile([P, 2], F32, name="sums_scaled")
+        total = sb.tile([P, 1], F32, name="total")
+        nc.scalar.activation(sums_scaled[:], sums[:], ACT.Copy, scale=1.0 / SLOTS, accum_out=total[:])
+        norm = sb.tile([P, 1], F32, name="norm")
+
+        nc.vector.tensor_copy(placed[:].indirect(half_offsets[0]), probs[0][:])
+        nc.vector.reciprocal(norm[:], total[:])
+        nc.vector.tensor_copy(placed[:].indirect(half_offsets[1]), probs[1][:])
+
+        decayed = sb.tile([P, T], F32, name="decayed", tag="reused")
+        result = sb.tile([P, T], F32, name="result")
+        start = 0
+        for width in OUT_WIDTHS:
+            cols = slice(start, start + width)
+            nc.scalar.activation(decayed[:, cols], mass_sb[:, cols], ACT.Copy, scale=dec_sb[:])
+            nc.vector.scalar_tensor_tensor(result[:, cols], placed[:, cols], norm[:], decayed[:, cols], ALU.mult, ALU.add)
+            nc.sync.dma_start(out[:, cols], result[:, cols])
+            start = start + width

@@ -17,7 +17,9 @@ ACT = mybir.ActivationFunctionType
 
 P = 128
 HALF = SLOTS // 2
-OUT_WIDTHS = (256, 512, 512, 512, 256)
+OUT_WIDTHS = (128, 384, 512, 512, 384, 128)
+FIRST_WORDS = 512
+HEADROOM = 64.0
 
 
 def tile_attend_heavyhitter_kernel(tc, query, keys_words, keys_scales, mass, dec, offs, out):
@@ -27,28 +29,30 @@ def tile_attend_heavyhitter_kernel(tc, query, keys_words, keys_scales, mass, dec
         ps = ctx.enter_context(tc.psum_pool(name="ps", bufs=1))
 
         offsets = sb.tile([P, SLOTS // 16], U16, name="offsets")
-        q_raw = sb.tile([P, 4, Q], F32, name="q_raw", tag="raw")
+        q_raw = sb.tile([P, 4, Q], F32, name="q_raw")
         pool_scales = sb.tile([P, T], U8, name="pool_scales", align_bytes=64)
         pool_words = sb.tile([P, T], I32, name="pool_words", align_bytes=64)
+        mass_sb = sb.tile([P, T], F32, name="mass_sb")
         dec_sb = sb.tile([P, 1], F32, name="dec_sb")
         placed = sb.tile([P, T], F32, name="placed")
 
         nc.vector.memset(pool_scales[:].bitcast(I32), 0)
         nc.sync.dma_start(offsets[:], offs)
-        nc.sync.dma_start(dec_sb[:], dec)
-        nc.sync.dma_start(q_raw[:], query.rearrange("(p j) q -> p j q", j=4))
+        words_hbm = keys_words[0].rearrange("p n t -> p (n t)").bitcast(I32)
+        nc.sync.dma_start(pool_words[:, :FIRST_WORDS], words_hbm[:, :FIRST_WORDS])
         for quad in range(4):
             nc.sync.dma_start(
                 pool_scales[32 * quad : 32 * quad + 4, :].bitcast(I32),
                 keys_scales[0, 4 * quad : 4 * quad + 4, :].bitcast(I32),
             )
-        nc.sync.dma_start(pool_words[:], keys_words[0].rearrange("p n t -> p (n t)").bitcast(I32))
+        nc.sync.dma_start(pool_words[:, FIRST_WORDS:], words_hbm[:, FIRST_WORDS:])
+        nc.sync.dma_start(q_raw[:], query.rearrange("(p j) q -> p j q", j=4))
+        nc.sync.dma_start(mass_sb[:], mass)
+        nc.sync.dma_start(dec_sb[:], dec)
         nc.vector.memset(placed[:], 0.0)
 
         q_bf = sb.tile([P, Q, 4], BF16, name="q_bf", align_bytes=64)
-        nc.scalar.copy(q_bf[:], q_raw[:].rearrange("p j q -> p q j"))
-        mass_sb = sb.tile([P, T], F32, name="mass_sb", tag="raw")
-        nc.sync.dma_start(mass_sb[:], mass)
+        nc.scalar.activation(q_bf[:], q_raw[:].rearrange("p j q -> p q j"), ACT.Copy, scale=-1.0)
         q_codes = sb.tile([P, Q], U32, name="q_codes", align_bytes=64)
         q_scales = sb.tile([P, Q], U8, name="q_scales", align_bytes=64)
         nc.vector.quantize_mx(
@@ -74,18 +78,18 @@ def tile_attend_heavyhitter_kernel(tc, query, keys_words, keys_scales, mass, dec
                 stop=True,
             )
 
-        neg_max_first = sb.tile([P, 1], F32, name="neg_max_first")
-        neg_max = sb.tile([P, 1], F32, name="neg_max")
-        nc.vector.tensor_reduce(neg_max_first[:], scores[0][:], mybir.AxisListType.X, ALU.max, negate=True)
-        neg_second = sb.tile([P, HALF], F32, name="neg_second", tag="reused")
+        shift_first = sb.tile([P, 1], F32, name="shift_first")
+        shift_second = sb.tile([P, 1], F32, name="shift_second", tag="reused")
+        raised = sb.tile([P, HALF], F32, name="raised")
+        nc.vector.tensor_reduce(shift_first[:], scores[0][:], mybir.AxisListType.X, ALU.min)
         nc.vector.tensor_scalar(
-            neg_second[:], scores[1][:], -1.0, neg_max_first[:], ALU.mult, ALU.min, accum_out=neg_max[:]
+            raised[:], scores[1][:], HEADROOM, shift_first[:], ALU.add, ALU.min, accum_out=shift_second[:]
         )
 
         sums = sb.tile([P, 2], F32, name="sums")
         probs = [sb.tile([P, HALF], F32, name="probs%d" % h) for h in range(2)]
-        nc.scalar.activation(probs[0][:], scores[0][:], ACT.Exp, bias=neg_max[:], scale=1.0, accum_out=sums[:, 0:1])
-        nc.scalar.activation(probs[1][:], neg_second[:], ACT.Exp, bias=neg_max[:], scale=-1.0, accum_out=sums[:, 1:2])
+        nc.scalar.activation(probs[0][:], scores[0][:], ACT.Exp, bias=shift_first[:], scale=-1.0, accum_out=sums[:, 0:1])
+        nc.scalar.activation(probs[1][:], scores[1][:], ACT.Exp, bias=shift_second[:], scale=-1.0, accum_out=sums[:, 1:2])
         sums_scaled = sb.tile([P, 2], F32, name="sums_scaled")
         total = sb.tile([P, 1], F32, name="total")
         nc.scalar.activation(sums_scaled[:], sums[:], ACT.Copy, scale=1.0 / SLOTS, accum_out=total[:])

@@ -37,13 +37,13 @@ def tile_attend_heavyhitter_kernel(tc, query, keys_words, keys_scales, mass, dec
         placed = sb.tile([P, T], F32, name="placed")
 
         nc.vector.memset(pool_scales[:].bitcast(I32), 0)
-        nc.sync.dma_start(offsets[:], offs)
         words_hbm = keys_words[0].rearrange("p n t -> p (n t)").bitcast(I32)
         nc.sync.dma_start(pool_words[:, :FIRST_WORDS], words_hbm[:, :FIRST_WORDS])
-        for quad in range(4):
+        nc.sync.dma_start(offsets[:], offs)
+        for r in range(4):
             nc.sync.dma_start(
-                pool_scales[32 * quad : 32 * quad + 4, :].bitcast(I32),
-                keys_scales[0, 4 * quad : 4 * quad + 4, :].bitcast(I32),
+                pool_scales[r:P:32, :].bitcast(I32),
+                keys_scales[0, r:16:4, :].bitcast(I32),
             )
         nc.sync.dma_start(pool_words[:, FIRST_WORDS:], words_hbm[:, FIRST_WORDS:])
         nc.sync.dma_start(q_raw[:], query.rearrange("(p j) q -> p j q", j=4))

@@ -17,7 +17,7 @@ ACT = mybir.ActivationFunctionType
 
 P = 128
 HALF = SLOTS // 2
-OUT_WIDTHS = (128, 384, 512, 512, 384, 128)
+OUT_WIDTHS = (128, 128, 256, 256, 256, 256, 256, 256, 256)
 FIRST_WORDS = 512
 HEADROOM = 64.0
 
@@ -38,15 +38,14 @@ def tile_attend_heavyhitter_kernel(tc, query, keys_words, keys_scales, mass, dec
 
         nc.vector.memset(pool_scales[:].bitcast(I32), 0)
         words_hbm = keys_words[0].rearrange("p n t -> p (n t)").bitcast(I32)
-        nc.sync.dma_start(pool_words[:, :FIRST_WORDS], words_hbm[:, :FIRST_WORDS])
+        nc.sync.dma_start(q_raw[:], query.rearrange("(p j) q -> p j q", j=4))
         nc.sync.dma_start(offsets[:], offs)
         for r in range(4):
             nc.sync.dma_start(
                 pool_scales[r:P:32, :].bitcast(I32),
                 keys_scales[0, r:16:4, :].bitcast(I32),
             )
-        nc.sync.dma_start(pool_words[:, FIRST_WORDS:], words_hbm[:, FIRST_WORDS:])
-        nc.sync.dma_start(q_raw[:], query.rearrange("(p j) q -> p j q", j=4))
+        nc.sync.dma_start(pool_words[:], words_hbm)
         nc.sync.dma_start(mass_sb[:], mass)
         nc.sync.dma_start(dec_sb[:], dec)
         nc.vector.memset(placed[:], 0.0)

@@ -16,10 +16,12 @@ ALU = mybir.AluOpType
 ACT = mybir.ActivationFunctionType
 
 P = 128
+PACK = 4
+GROUP = 16
 HALF = SLOTS // 2
-OUT_WIDTHS = (128, 128, 256, 256, 256, 256, 256, 256, 256)
-FIRST_WORDS = 512
+WEIGHT_UNITS = 512.0
 HEADROOM = 64.0
+OUT_WIDTHS = (128, 128) + (256,) * 7
 
 
 def tile_attend_heavyhitter_kernel(tc, query, keys_words, keys_scales, mass, dec, offs, out):
@@ -28,30 +30,29 @@ def tile_attend_heavyhitter_kernel(tc, query, keys_words, keys_scales, mass, dec
         sb = ctx.enter_context(tc.tile_pool(name="sb", bufs=1))
         ps = ctx.enter_context(tc.psum_pool(name="ps", bufs=1))
 
-        offsets = sb.tile([P, SLOTS // 16], U16, name="offsets")
-        q_raw = sb.tile([P, 4, Q], F32, name="q_raw")
+        offsets = sb.tile([P, SLOTS // GROUP], U16, name="offsets")
+        q_raw = sb.tile([P, PACK, Q], F32, name="q_raw", tag="query_then_mass")
         pool_scales = sb.tile([P, T], U8, name="pool_scales", align_bytes=64)
         pool_words = sb.tile([P, T], I32, name="pool_words", align_bytes=64)
-        mass_sb = sb.tile([P, T], F32, name="mass_sb")
         dec_sb = sb.tile([P, 1], F32, name="dec_sb")
         placed = sb.tile([P, T], F32, name="placed")
 
         nc.vector.memset(pool_scales[:].bitcast(I32), 0)
-        words_hbm = keys_words[0].rearrange("p n t -> p (n t)").bitcast(I32)
-        nc.sync.dma_start(q_raw[:], query.rearrange("(p j) q -> p j q", j=4))
+        nc.sync.dma_start(q_raw[:], query.rearrange("(p j) q -> p j q", j=PACK))
         nc.sync.dma_start(offsets[:], offs)
-        for r in range(4):
+        for r in range(PACK):
             nc.sync.dma_start(
                 pool_scales[r:P:32, :].bitcast(I32),
-                keys_scales[0, r:16:4, :].bitcast(I32),
+                keys_scales[0, r : D // 32 : PACK, :].bitcast(I32),
             )
-        nc.sync.dma_start(pool_words[:], words_hbm)
-        nc.sync.dma_start(mass_sb[:], mass)
+        nc.sync.dma_start(pool_words[:], keys_words[0].rearrange("p n t -> p (n t)").bitcast(I32))
         nc.sync.dma_start(dec_sb[:], dec)
         nc.vector.memset(placed[:], 0.0)
 
-        q_bf = sb.tile([P, Q, 4], BF16, name="q_bf", align_bytes=64)
+        q_bf = sb.tile([P, Q, PACK], BF16, name="q_bf", align_bytes=64)
         nc.scalar.activation(q_bf[:], q_raw[:].rearrange("p j q -> p q j"), ACT.Copy, scale=-1.0)
+        mass_sb = sb.tile([P, T], F32, name="mass_sb", tag="query_then_mass")
+        nc.sync.dma_start(mass_sb[:], mass)
         q_codes = sb.tile([P, Q], U32, name="q_codes", align_bytes=64)
         q_scales = sb.tile([P, Q], U8, name="q_scales", align_bytes=64)
         nc.vector.quantize_mx(
@@ -62,13 +63,13 @@ def tile_attend_heavyhitter_kernel(tc, query, keys_words, keys_scales, mass, dec
         nc.vector.tensor_copy(k_scales[:], pool_scales[:].indirect(offsets[:]))
 
         halves = [slice(h * HALF, (h + 1) * HALF) for h in range(2)]
-        half_offsets = [offsets[:, h * HALF // 16 : (h + 1) * HALF // 16] for h in range(2)]
+        half_offsets = [offsets[:, h * HALF // GROUP : (h + 1) * HALF // GROUP] for h in range(2)]
         k_words = [sb.tile([P, HALF], U32, name="k_words%d" % h, align_bytes=64) for h in range(2)]
-        scores = [ps.tile([P, HALF], F32, name="scores%d" % h) for h in range(2)]
+        neg_scores = [ps.tile([P, HALF], F32, name="neg_scores%d" % h) for h in range(2)]
         for h in range(2):
             nc.vector.tensor_copy(k_words[h][:], pool_words[:].bitcast(U32).indirect(half_offsets[h]))
             nc.tensor.matmul_mx(
-                out=scores[h][:],
+                out=neg_scores[h][:],
                 lhsT=q_codes[:].bitcast(FP8X4),
                 lhsT_scale=q_scales[:],
                 rhs=k_words[h][:].bitcast(FP8X4),
@@ -77,33 +78,37 @@ def tile_attend_heavyhitter_kernel(tc, query, keys_words, keys_scales, mass, dec
                 stop=True,
             )
 
-        shift_first = sb.tile([P, 1], F32, name="shift_first")
-        shift_second = sb.tile([P, 1], F32, name="shift_second", tag="reused")
+        bias_first = sb.tile([P, 1], F32, name="bias_first")
+        bias_second = sb.tile([P, 1], F32, name="bias_second", tag="bias_then_decayed")
         raised = sb.tile([P, HALF], F32, name="raised")
-        nc.vector.tensor_reduce(shift_first[:], scores[0][:], mybir.AxisListType.X, ALU.min)
+        nc.vector.tensor_reduce(bias_first[:], neg_scores[0][:], mybir.AxisListType.X, ALU.min)
         nc.vector.tensor_scalar(
-            raised[:], scores[1][:], HEADROOM, shift_first[:], ALU.add, ALU.min, accum_out=shift_second[:]
+            raised[:], neg_scores[1][:], HEADROOM, bias_first[:], ALU.add, ALU.min, accum_out=bias_second[:]
         )
 
         sums = sb.tile([P, 2], F32, name="sums")
         probs = [sb.tile([P, HALF], F32, name="probs%d" % h) for h in range(2)]
-        nc.scalar.activation(probs[0][:], scores[0][:], ACT.Exp, bias=shift_first[:], scale=-1.0, accum_out=sums[:, 0:1])
-        nc.scalar.activation(probs[1][:], scores[1][:], ACT.Exp, bias=shift_second[:], scale=-1.0, accum_out=sums[:, 1:2])
+        for h, bias in enumerate((bias_first, bias_second)):
+            nc.scalar.activation(
+                probs[h][:], neg_scores[h][:], ACT.Exp, bias=bias[:], scale=-1.0, accum_out=sums[:, h : h + 1]
+            )
         sums_scaled = sb.tile([P, 2], F32, name="sums_scaled")
         total = sb.tile([P, 1], F32, name="total")
-        nc.scalar.activation(sums_scaled[:], sums[:], ACT.Copy, scale=1.0 / SLOTS, accum_out=total[:])
+        nc.scalar.activation(sums_scaled[:], sums[:], ACT.Copy, scale=1.0 / WEIGHT_UNITS, accum_out=total[:])
         norm = sb.tile([P, 1], F32, name="norm")
 
         nc.vector.tensor_copy(placed[:].indirect(half_offsets[0]), probs[0][:])
         nc.vector.reciprocal(norm[:], total[:])
         nc.vector.tensor_copy(placed[:].indirect(half_offsets[1]), probs[1][:])
 
-        decayed = sb.tile([P, T], F32, name="decayed", tag="reused")
+        decayed = sb.tile([P, T], F32, name="decayed", tag="bias_then_decayed")
         result = sb.tile([P, T], F32, name="result")
-        start = 0
+        first = 0
         for width in OUT_WIDTHS:
-            cols = slice(start, start + width)
+            cols = slice(first, first + width)
             nc.scalar.activation(decayed[:, cols], mass_sb[:, cols], ACT.Copy, scale=dec_sb[:])
-            nc.vector.scalar_tensor_tensor(result[:, cols], placed[:, cols], norm[:], decayed[:, cols], ALU.mult, ALU.add)
+            nc.vector.scalar_tensor_tensor(
+                result[:, cols], placed[:, cols], norm[:], decayed[:, cols], ALU.mult, ALU.add
+            )
             nc.sync.dma_start(out[:, cols], result[:, cols])
-            start = start + width
+            first = first + width

@@ -19,6 +19,7 @@ P = 128
 PACK = 4
 GROUP = 16
 HALF = SLOTS // 2
+SPREAD = P // (D // 32)
 WEIGHT_UNITS = 512.0
 HEADROOM = 64.0
 OUT_WIDTHS = (128, 128) + (256,) * 7
@@ -31,36 +32,39 @@ def tile_attend_heavyhitter_kernel(tc, query, keys_words, keys_scales, mass, dec
         ps = ctx.enter_context(tc.psum_pool(name="ps", bufs=1))
 
         offsets = sb.tile([P, SLOTS // GROUP], U16, name="offsets")
-        q_raw = sb.tile([P, PACK, Q], F32, name="q_raw", tag="query_then_mass")
-        pool_scales = sb.tile([P, T], U8, name="pool_scales", align_bytes=64)
+        q_raw = sb.tile([P, PACK, Q], F32, name="q_raw")
+        pool_scales = sb.tile([P, T], U8, name="pool_scales", tag="scales_then_dec", align_bytes=64)
+        k_scales = sb.tile([P, SLOTS], U8, name="k_scales", align_bytes=64)
         pool_words = sb.tile([P, T], I32, name="pool_words", align_bytes=64)
-        dec_sb = sb.tile([P, 1], F32, name="dec_sb")
         placed = sb.tile([P, T], F32, name="placed")
 
         nc.vector.memset(pool_scales[:].bitcast(I32), 0)
         nc.sync.dma_start(q_raw[:], query.rearrange("(p j) q -> p j q", j=PACK))
         nc.sync.dma_start(offsets[:], offs)
-        for r in range(PACK):
-            nc.sync.dma_start(
-                pool_scales[r:P:32, :].bitcast(I32),
-                keys_scales[0, r : D // 32 : PACK, :].bitcast(I32),
-            )
+        nc.sync.dma_start(pool_scales[SPREAD // 2 : P : SPREAD, :].bitcast(I32), keys_scales[0].bitcast(I32))
         nc.sync.dma_start(pool_words[:], keys_words[0].rearrange("p n t -> p (n t)").bitcast(I32))
-        nc.sync.dma_start(dec_sb[:], dec)
         nc.vector.memset(placed[:], 0.0)
+        nc.vector.memset(k_scales[:].bitcast(I32), 0)
 
-        q_bf = sb.tile([P, Q, PACK], BF16, name="q_bf", align_bytes=64)
+        q_bf = sb.tile([P, Q, PACK], BF16, name="q_bf", tag="cast_then_mass", align_bytes=64)
         nc.scalar.activation(q_bf[:], q_raw[:].rearrange("p j q -> p q j"), ACT.Copy, scale=-1.0)
-        mass_sb = sb.tile([P, T], F32, name="mass_sb", tag="query_then_mass")
-        nc.sync.dma_start(mass_sb[:], mass)
         q_codes = sb.tile([P, Q], U32, name="q_codes", align_bytes=64)
         q_scales = sb.tile([P, Q], U8, name="q_scales", align_bytes=64)
         nc.vector.quantize_mx(
             out=q_codes[:].bitcast(FP8X4), scales=q_scales[:], in_=q_bf[:].rearrange("p q j -> p (q j)")
         )
 
-        k_scales = sb.tile([P, SLOTS], U8, name="k_scales", align_bytes=64)
-        nc.vector.tensor_copy(k_scales[:], pool_scales[:].indirect(offsets[:]))
+        spread_scales = sb.tile([P, SLOTS], U8, name="spread_scales", align_bytes=64)
+        nc.vector.tensor_copy(spread_scales[:], pool_scales[:].indirect(offsets[:]))
+        for r in range(PACK):
+            nc.sync.dma_start(
+                k_scales[r:P:32, :].bitcast(I32),
+                spread_scales[SPREAD * r + SPREAD // 2 : P : 32, :].bitcast(I32),
+            )
+        dec_sb = sb.tile([P, 1], F32, name="dec_sb", tag="scales_then_dec", align_bytes=64)
+        nc.sync.dma_start(dec_sb[:], dec)
+        mass_sb = sb.tile([P, T], F32, name="mass_sb", tag="cast_then_mass", align_bytes=64)
+        nc.sync.dma_start(mass_sb[:], mass)
 
         halves = [slice(h * HALF, (h + 1) * HALF) for h in range(2)]
         half_offsets = [offsets[:, h * HALF // GROUP : (h + 1) * HALF // GROUP] for h in range(2)]

@@ -57,7 +57,7 @@ def tile_attend_heavyhitter_kernel(tc, query, keys_words, keys_scales, mass, dec
         spread_scales = sb.tile([P, SLOTS], U8, name="spread_scales", align_bytes=64)
         nc.vector.tensor_copy(spread_scales[:], pool_scales[:].indirect(offsets[:]))
         for r in range(PACK):
-            nc.sync.dma_start(
+            (nc.sync if r % 2 == 0 else nc.scalar).dma_start(
                 k_scales[r:P:32, :].bitcast(I32),
                 spread_scales[SPREAD * r + SPREAD // 2 : P : 32, :].bitcast(I32),
             )

@@ -21,7 +21,6 @@ GROUP = 16
 HALF = SLOTS // 2
 SPREAD = P // (D // 32)
 WEIGHT_UNITS = 512.0
-HEADROOM = 64.0
 OUT_WIDTHS = (128, 128) + (256,) * 7
 
 
@@ -37,12 +36,13 @@ def tile_attend_heavyhitter_kernel(tc, query, keys_words, keys_scales, mass, dec
         k_scales = sb.tile([P, SLOTS], U8, name="k_scales", align_bytes=64)
         pool_words = sb.tile([P, T], I32, name="pool_words", align_bytes=64)
         placed = sb.tile([P, T], F32, name="placed")
+        words_hbm = keys_words[0].rearrange("p n t -> p (n t)").bitcast(I32)
 
         nc.vector.memset(pool_scales[:].bitcast(I32), 0)
         nc.sync.dma_start(q_raw[:], query.rearrange("(p j) q -> p j q", j=PACK))
         nc.sync.dma_start(offsets[:], offs)
-        nc.sync.dma_start(pool_scales[SPREAD // 2 : P : SPREAD, :].bitcast(I32), keys_scales[0].bitcast(I32))
-        nc.sync.dma_start(pool_words[:], keys_words[0].rearrange("p n t -> p (n t)").bitcast(I32))
+        nc.sync.dma_start(pool_scales[11 : 11 + 7 * 16 : 7, :].bitcast(I32), keys_scales[0].bitcast(I32))
+        nc.sync.dma_start(pool_words[:], words_hbm)
         nc.vector.memset(placed[:], 0.0)
         nc.vector.memset(k_scales[:].bitcast(I32), 0)
 
@@ -53,57 +53,78 @@ def tile_attend_heavyhitter_kernel(tc, query, keys_words, keys_scales, mass, dec
         nc.vector.quantize_mx(
             out=q_codes[:].bitcast(FP8X4), scales=q_scales[:], in_=q_bf[:].rearrange("p q j -> p (q j)")
         )
-
         spread_scales = sb.tile([P, SLOTS], U8, name="spread_scales", align_bytes=64)
         nc.vector.tensor_copy(spread_scales[:], pool_scales[:].indirect(offsets[:]))
         for r in range(PACK):
             (nc.sync if r % 2 == 0 else nc.scalar).dma_start(
                 k_scales[r:P:32, :].bitcast(I32),
-                spread_scales[SPREAD * r + SPREAD // 2 : P : 32, :].bitcast(I32),
+                spread_scales[11 + 7 * r : 11 + 7 * 16 : 7 * PACK, :].bitcast(I32),
             )
         dec_sb = sb.tile([P, 1], F32, name="dec_sb", tag="scales_then_dec", align_bytes=64)
         nc.sync.dma_start(dec_sb[:], dec)
         mass_sb = sb.tile([P, T], F32, name="mass_sb", tag="cast_then_mass", align_bytes=64)
         nc.sync.dma_start(mass_sb[:], mass)
 
-        halves = [slice(h * HALF, (h + 1) * HALF) for h in range(2)]
-        half_offsets = [offsets[:, h * HALF // GROUP : (h + 1) * HALF // GROUP] for h in range(2)]
+        def listed(first, last):
+            return offsets[:, first // GROUP : last // GROUP]
+
         k_words = [sb.tile([P, HALF], U32, name="k_words%d" % h, align_bytes=64) for h in range(2)]
-        neg_scores = [ps.tile([P, HALF], F32, name="neg_scores%d" % h) for h in range(2)]
-        for h in range(2):
-            nc.vector.tensor_copy(k_words[h][:], pool_words[:].bitcast(U32).indirect(half_offsets[h]))
+
+        def gather_words(h):
+            nc.vector.tensor_copy(k_words[h][:], pool_words[:].bitcast(U32).indirect(listed(h * HALF, (h + 1) * HALF)))
+
+        def multiply(bank_cols, first, last):
+            h = first // HALF
             nc.tensor.matmul_mx(
-                out=neg_scores[h][:],
+                out=bank_cols,
                 lhsT=q_codes[:].bitcast(FP8X4),
                 lhsT_scale=q_scales[:],
-                rhs=k_words[h][:].bitcast(FP8X4),
-                rhs_scale=k_scales[:, halves[h]],
+                rhs=k_words[h][:, first - h * HALF : last - h * HALF].bitcast(FP8X4),
+                rhs_scale=k_scales[:, first:last],
                 start=True,
                 stop=True,
             )
 
-        bias_first = sb.tile([P, 1], F32, name="bias_first")
-        bias_second = sb.tile([P, 1], F32, name="bias_second", tag="bias_then_decayed")
-        raised = sb.tile([P, HALF], F32, name="raised")
-        nc.vector.tensor_reduce(bias_first[:], neg_scores[0][:], mybir.AxisListType.X, ALU.min)
-        nc.vector.tensor_scalar(
-            raised[:], neg_scores[1][:], HEADROOM, bias_first[:], ALU.add, ALU.min, accum_out=bias_second[:]
-        )
+        bounds = (0, 64, HALF, SLOTS)
+        widths = [bounds[i + 1] - bounds[i] for i in range(3)]
+        neg_scores = [ps.tile([P, widths[i]], F32, name="neg_scores%d" % i) for i in range(3)]
+        gather_words(0)
+        multiply(neg_scores[0][:], 0, 64)
+        multiply(neg_scores[1][:, 0:64], 64, 128)
+        multiply(neg_scores[1][:, 64:192], 128, 256)
+        gather_words(1)
+        multiply(neg_scores[2][:], HALF, SLOTS)
+        bias = [sb.tile([P, 1], F32, name="bias0", tag="bias_then_raised"), sb.tile([P, 1], F32, name="bias1"),
+                sb.tile([P, 1], F32, name="bias2", tag="bias_then_decayed")]
+        sums = sb.tile([P, 3], F32, name="sums")
+        probs = [sb.tile([P, widths[0]], F32, name="probs0"),
+                 sb.tile([P, widths[1]], F32, name="probs1"), sb.tile([P, widths[2]], F32, name="probs2")]
+        raised1 = sb.tile([P, widths[1]], F32, name="raised1")
 
-        sums = sb.tile([P, 2], F32, name="sums")
-        probs = [sb.tile([P, HALF], F32, name="probs%d" % h) for h in range(2)]
-        for h, bias in enumerate((bias_first, bias_second)):
+        def weigh(i):
             nc.scalar.activation(
-                probs[h][:], neg_scores[h][:], ACT.Exp, bias=bias[:], scale=-1.0, accum_out=sums[:, h : h + 1]
+                probs[i][:], neg_scores[i][:], ACT.Exp, bias=bias[i][:], scale=-1.0, accum_out=sums[:, i : i + 1]
             )
-        sums_scaled = sb.tile([P, 2], F32, name="sums_scaled")
-        total = sb.tile([P, 1], F32, name="total")
-        nc.scalar.activation(sums_scaled[:], sums[:], ACT.Copy, scale=1.0 / WEIGHT_UNITS, accum_out=total[:])
-        norm = sb.tile([P, 1], F32, name="norm")
 
-        nc.vector.tensor_copy(placed[:].indirect(half_offsets[0]), probs[0][:])
+        nc.vector.tensor_reduce(bias[0][:], neg_scores[0][:], mybir.AxisListType.X, ALU.min)
+        weigh(0)
+        nc.vector.tensor_scalar(
+            raised1[:], neg_scores[1][:], 32.0, bias[0][:], ALU.add, ALU.min, accum_out=bias[1][:]
+        )
+        weigh(1)
+        nc.vector.tensor_tensor(placed[:].indirect(listed(0, bounds[1])), probs[0][:], probs[0][:], ALU.add)
+        raised2 = sb.tile([P, widths[2]], F32, name="raised2", tag="bias_then_raised")
+        nc.vector.tensor_scalar(
+            raised2[:], neg_scores[2][:], 64.0, bias[1][:], ALU.add, ALU.min, accum_out=bias[2][:]
+        )
+        weigh(2)
+        nc.vector.tensor_tensor(placed[:].indirect(listed(bounds[1], HALF)), probs[1][:], probs[1][:], ALU.add)
+        sums_scaled = sb.tile([P, 3], F32, name="sums_scaled")
+        total = sb.tile([P, 1], F32, name="total")
+        nc.scalar.activation(sums_scaled[:], sums[:], ACT.Copy, scale=2.0 / WEIGHT_UNITS, accum_out=total[:])
+        norm = sb.tile([P, 1], F32, name="norm")
         nc.vector.reciprocal(norm[:], total[:])
-        nc.vector.tensor_copy(placed[:].indirect(half_offsets[1]), probs[1][:])
+        nc.vector.tensor_tensor(placed[:].indirect(listed(HALF, SLOTS)), probs[2][:], probs[2][:], ALU.add)
 
         decayed = sb.tile([P, T], F32, name="decayed", tag="bias_then_decayed")
         result = sb.tile([P, T], F32, name="result")

@@ -28,12 +28,13 @@ def tile_attend_heavyhitter_kernel(tc, query, keys_words, keys_scales, mass, dec
     nc = tc.nc
     with ExitStack() as ctx:
         sb = ctx.enter_context(tc.tile_pool(name="sb", bufs=1))
+        shared = ctx.enter_context(tc.tile_pool(name="shared", bufs=1))
         ps = ctx.enter_context(tc.psum_pool(name="ps", bufs=1))
 
         offsets = sb.tile([P, SLOTS // GROUP], U16, name="offsets")
         q_raw = sb.tile([P, PACK, Q], F32, name="q_raw")
-        pool_scales = sb.tile([P, T], U8, name="pool_scales", tag="scales_then_dec", align_bytes=64)
-        k_scales = sb.tile([P, SLOTS], U8, name="k_scales", align_bytes=64)
+        pool_scales = shared.tile([P, T], U8, name="pool_scales", align_bytes=64, offset=0)
+        k_scales = [sb.tile([P, HALF], U8, name="k_scales%d" % h, align_bytes=64) for h in range(2)]
         pool_words = sb.tile([P, T], I32, name="pool_words", align_bytes=64)
         placed = sb.tile([P, T], F32, name="placed")
         words_hbm = keys_words[0].rearrange("p n t -> p (n t)").bitcast(I32)
@@ -44,23 +45,27 @@ def tile_attend_heavyhitter_kernel(tc, query, keys_words, keys_scales, mass, dec
         nc.sync.dma_start(pool_scales[11 : 11 + 7 * 16 : 7, :].bitcast(I32), keys_scales[0].bitcast(I32))
         nc.sync.dma_start(pool_words[:], words_hbm)
         nc.vector.memset(placed[:], 0.0)
-        nc.vector.memset(k_scales[:].bitcast(I32), 0)
+        for h in range(2):
+            nc.vector.memset(k_scales[h][:].bitcast(I32), 0)
 
+        for h in range(2):
+            spread_scales = sb.tile([P, HALF], U8, name="spread_scales%d" % h, align_bytes=64)
+            nc.vector.tensor_copy(
+                spread_scales[:], pool_scales[:].indirect(offsets[:, h * HALF // GROUP : (h + 1) * HALF // GROUP])
+            )
+            for r in range(PACK):
+                nc.sync.dma_start(
+                    k_scales[h][r:P:32, :].bitcast(I32),
+                    spread_scales[11 + 7 * r : 11 + 7 * 16 : 7 * PACK, :].bitcast(I32),
+                )
         q_bf = sb.tile([P, Q, PACK], BF16, name="q_bf", tag="cast_then_mass", align_bytes=64)
         nc.scalar.activation(q_bf[:], q_raw[:].rearrange("p j q -> p q j"), ACT.Copy, scale=-1.0)
-        q_codes = sb.tile([P, Q], U32, name="q_codes", align_bytes=64)
+        q_codes = shared.tile([P, Q], U32, name="q_codes", align_bytes=64, offset=0)
         q_scales = sb.tile([P, Q], U8, name="q_scales", align_bytes=64)
         nc.vector.quantize_mx(
             out=q_codes[:].bitcast(FP8X4), scales=q_scales[:], in_=q_bf[:].rearrange("p q j -> p (q j)")
         )
-        spread_scales = sb.tile([P, SLOTS], U8, name="spread_scales", align_bytes=64)
-        nc.vector.tensor_copy(spread_scales[:], pool_scales[:].indirect(offsets[:]))
-        for r in range(PACK):
-            (nc.sync if r % 2 == 0 else nc.scalar).dma_start(
-                k_scales[r:P:32, :].bitcast(I32),
-                spread_scales[11 + 7 * r : 11 + 7 * 16 : 7 * PACK, :].bitcast(I32),
-            )
-        dec_sb = sb.tile([P, 1], F32, name="dec_sb", tag="scales_then_dec", align_bytes=64)
+        dec_sb = shared.tile([P, 1], F32, name="dec_sb", align_bytes=64, offset=T // 2)
         nc.sync.dma_start(dec_sb[:], dec)
         mass_sb = sb.tile([P, T], F32, name="mass_sb", tag="cast_then_mass", align_bytes=64)
         nc.sync.dma_start(mass_sb[:], mass)
@@ -68,7 +73,7 @@ def tile_attend_heavyhitter_kernel(tc, query, keys_words, keys_scales, mass, dec
         def listed(first, last):
             return offsets[:, first // GROUP : last // GROUP]
 
-        k_words = [sb.tile([P, HALF], U32, name="k_words%d" % h, align_bytes=64) for h in range(2)]
+        k_words = [sb.tile([P, HALF], U32, name="k_words%d" % h, tag="k_words%d" % h, align_bytes=64) for h in range(2)]
 
         def gather_words(h):
             nc.vector.tensor_copy(k_words[h][:], pool_words[:].bitcast(U32).indirect(listed(h * HALF, (h + 1) * HALF)))
@@ -80,7 +85,7 @@ def tile_attend_heavyhitter_kernel(tc, query, keys_words, keys_scales, mass, dec
                 lhsT=q_codes[:].bitcast(FP8X4),
                 lhsT_scale=q_scales[:],
                 rhs=k_words[h][:, first - h * HALF : last - h * HALF].bitcast(FP8X4),
-                rhs_scale=k_scales[:, first:last],
+                rhs_scale=k_scales[h][:, first - h * HALF : last - h * HALF],
                 start=True,
                 stop=True,
             )
@@ -98,7 +103,8 @@ def tile_attend_heavyhitter_kernel(tc, query, keys_words, keys_scales, mass, dec
                 sb.tile([P, 1], F32, name="bias2", tag="bias_then_decayed")]
         sums = sb.tile([P, 3], F32, name="sums")
         probs = [sb.tile([P, widths[0]], F32, name="probs0"),
-                 sb.tile([P, widths[1]], F32, name="probs1"), sb.tile([P, widths[2]], F32, name="probs2")]
+                 sb.tile([P, widths[1]], F32, name="probs1", tag="k_words1", align_bytes=64),
+                 sb.tile([P, widths[2]], F32, name="probs2")]
         raised1 = sb.tile([P, widths[1]], F32, name="raised1")
 
         def weigh(i):

@@ -16,11 +16,17 @@ ALU = mybir.AluOpType
 ACT = mybir.ActivationFunctionType
 
 P = 128
+QUADRANT = 32
 PACK = 4
 GROUP = 16
 HALF = SLOTS // 2
-SPREAD = P // (D // 32)
+SCALE_ROWS = D // 32
+ROW_FIRST, ROW_STEP = 11, 7
+ROW_END = ROW_FIRST + ROW_STEP * SCALE_ROWS
+FIRST = 64
+PIECES = ((0, FIRST), (FIRST, HALF), (HALF, SLOTS))
 WEIGHT_UNITS = 512.0
+HEADROOM_STEP = 32.0
 OUT_WIDTHS = (128, 128) + (256,) * 7
 
 
@@ -37,27 +43,28 @@ def tile_attend_heavyhitter_kernel(tc, query, keys_words, keys_scales, mass, dec
         k_scales = [sb.tile([P, HALF], U8, name="k_scales%d" % h, align_bytes=64) for h in range(2)]
         pool_words = sb.tile([P, T], I32, name="pool_words", align_bytes=64)
         placed = sb.tile([P, T], F32, name="placed")
-        words_hbm = keys_words[0].rearrange("p n t -> p (n t)").bitcast(I32)
+
+        def listed(first, last):
+            return offsets[:, first // GROUP : last // GROUP]
 
         nc.vector.memset(pool_scales[:].bitcast(I32), 0)
         nc.sync.dma_start(q_raw[:], query.rearrange("(p j) q -> p j q", j=PACK))
         nc.sync.dma_start(offsets[:], offs)
-        nc.sync.dma_start(pool_scales[11 : 11 + 7 * 16 : 7, :].bitcast(I32), keys_scales[0].bitcast(I32))
-        nc.sync.dma_start(pool_words[:], words_hbm)
-        nc.vector.memset(placed[:], 0.0)
+        nc.sync.dma_start(pool_scales[ROW_FIRST:ROW_END:ROW_STEP, :].bitcast(I32), keys_scales[0].bitcast(I32))
+        nc.sync.dma_start(pool_words[:], keys_words[0].rearrange("p n t -> p (n t)").bitcast(I32))
+        nc.vector.memset(placed[:].bitcast(I32), 0)
         for h in range(2):
             nc.vector.memset(k_scales[h][:].bitcast(I32), 0)
 
         for h in range(2):
             spread_scales = sb.tile([P, HALF], U8, name="spread_scales%d" % h, align_bytes=64)
-            nc.vector.tensor_copy(
-                spread_scales[:], pool_scales[:].indirect(offsets[:, h * HALF // GROUP : (h + 1) * HALF // GROUP])
-            )
+            nc.vector.tensor_copy(spread_scales[:], pool_scales[:].indirect(listed(h * HALF, (h + 1) * HALF)))
             for r in range(PACK):
                 nc.sync.dma_start(
-                    k_scales[h][r:P:32, :].bitcast(I32),
-                    spread_scales[11 + 7 * r : 11 + 7 * 16 : 7 * PACK, :].bitcast(I32),
+                    k_scales[h][r:P:QUADRANT, :].bitcast(I32),
+                    spread_scales[ROW_FIRST + ROW_STEP * r : ROW_END : ROW_STEP * PACK, :].bitcast(I32),
                 )
+
         q_bf = sb.tile([P, Q, PACK], BF16, name="q_bf", tag="cast_then_mass", align_bytes=64)
         nc.scalar.activation(q_bf[:], q_raw[:].rearrange("p j q -> p q j"), ACT.Copy, scale=-1.0)
         q_codes = shared.tile([P, Q], U32, name="q_codes", align_bytes=64, offset=0)
@@ -70,67 +77,77 @@ def tile_attend_heavyhitter_kernel(tc, query, keys_words, keys_scales, mass, dec
         mass_sb = sb.tile([P, T], F32, name="mass_sb", tag="cast_then_mass", align_bytes=64)
         nc.sync.dma_start(mass_sb[:], mass)
 
-        def listed(first, last):
-            return offsets[:, first // GROUP : last // GROUP]
-
-        k_words = [sb.tile([P, HALF], U32, name="k_words%d" % h, tag="k_words%d" % h, align_bytes=64) for h in range(2)]
+        k_words = [
+            sb.tile([P, HALF], U32, name="k_words0", align_bytes=64),
+            sb.tile([P, HALF], U32, name="k_words1", tag="words_then_probs", align_bytes=64),
+        ]
+        widths = [last - first for first, last in PIECES]
+        neg_scores = [ps.tile([P, width], F32, name="neg_scores%d" % i) for i, width in enumerate(widths)]
 
         def gather_words(h):
             nc.vector.tensor_copy(k_words[h][:], pool_words[:].bitcast(U32).indirect(listed(h * HALF, (h + 1) * HALF)))
 
-        def multiply(bank_cols, first, last):
+        def multiply(i, first, last):
             h = first // HALF
+            in_half = slice(first - h * HALF, last - h * HALF)
             nc.tensor.matmul_mx(
-                out=bank_cols,
+                out=neg_scores[i][:, first - PIECES[i][0] : last - PIECES[i][0]],
                 lhsT=q_codes[:].bitcast(FP8X4),
                 lhsT_scale=q_scales[:],
-                rhs=k_words[h][:, first - h * HALF : last - h * HALF].bitcast(FP8X4),
-                rhs_scale=k_scales[h][:, first - h * HALF : last - h * HALF],
+                rhs=k_words[h][:, in_half].bitcast(FP8X4),
+                rhs_scale=k_scales[h][:, in_half],
                 start=True,
                 stop=True,
             )
 
-        bounds = (0, 64, HALF, SLOTS)
-        widths = [bounds[i + 1] - bounds[i] for i in range(3)]
-        neg_scores = [ps.tile([P, widths[i]], F32, name="neg_scores%d" % i) for i in range(3)]
         gather_words(0)
-        multiply(neg_scores[0][:], 0, 64)
-        multiply(neg_scores[1][:, 0:64], 64, 128)
-        multiply(neg_scores[1][:, 64:192], 128, 256)
+        multiply(0, 0, FIRST)
+        multiply(1, FIRST, 2 * FIRST)
+        multiply(1, 2 * FIRST, HALF)
         gather_words(1)
-        multiply(neg_scores[2][:], HALF, SLOTS)
-        bias = [sb.tile([P, 1], F32, name="bias0", tag="bias_then_raised"), sb.tile([P, 1], F32, name="bias1"),
-                sb.tile([P, 1], F32, name="bias2", tag="bias_then_decayed")]
-        sums = sb.tile([P, 3], F32, name="sums")
-        probs = [sb.tile([P, widths[0]], F32, name="probs0"),
-                 sb.tile([P, widths[1]], F32, name="probs1", tag="k_words1", align_bytes=64),
-                 sb.tile([P, widths[2]], F32, name="probs2")]
-        raised1 = sb.tile([P, widths[1]], F32, name="raised1")
+        multiply(2, HALF, SLOTS)
+
+        bias = [
+            sb.tile([P, 1], F32, name="bias0", tag="bias_then_raised"),
+            sb.tile([P, 1], F32, name="bias1"),
+            sb.tile([P, 1], F32, name="bias2", tag="bias_then_decayed"),
+        ]
+        sums = sb.tile([P, len(PIECES)], F32, name="sums")
+        probs = [
+            sb.tile([P, widths[0]], F32, name="probs0"),
+            sb.tile([P, widths[1]], F32, name="probs1", tag="words_then_probs", align_bytes=64),
+            sb.tile([P, widths[2]], F32, name="probs2"),
+        ]
+
+        def chain_bias(i, raised):
+            nc.vector.tensor_scalar(
+                raised[:], neg_scores[i][:], i * HEADROOM_STEP, bias[i - 1][:], ALU.add, ALU.min, accum_out=bias[i][:]
+            )
 
         def weigh(i):
             nc.scalar.activation(
                 probs[i][:], neg_scores[i][:], ACT.Exp, bias=bias[i][:], scale=-1.0, accum_out=sums[:, i : i + 1]
             )
 
+        def place(i):
+            nc.vector.tensor_tensor(placed[:].indirect(listed(*PIECES[i])), probs[i][:], probs[i][:], ALU.add)
+
+        raised1 = sb.tile([P, widths[1]], F32, name="raised1")
         nc.vector.tensor_reduce(bias[0][:], neg_scores[0][:], mybir.AxisListType.X, ALU.min)
         weigh(0)
-        nc.vector.tensor_scalar(
-            raised1[:], neg_scores[1][:], 32.0, bias[0][:], ALU.add, ALU.min, accum_out=bias[1][:]
-        )
+        chain_bias(1, raised1)
         weigh(1)
-        nc.vector.tensor_tensor(placed[:].indirect(listed(0, bounds[1])), probs[0][:], probs[0][:], ALU.add)
+        place(0)
         raised2 = sb.tile([P, widths[2]], F32, name="raised2", tag="bias_then_raised")
-        nc.vector.tensor_scalar(
-            raised2[:], neg_scores[2][:], 64.0, bias[1][:], ALU.add, ALU.min, accum_out=bias[2][:]
-        )
+        chain_bias(2, raised2)
         weigh(2)
-        nc.vector.tensor_tensor(placed[:].indirect(listed(bounds[1], HALF)), probs[1][:], probs[1][:], ALU.add)
-        sums_scaled = sb.tile([P, 3], F32, name="sums_scaled")
+        place(1)
+        sums_scaled = sb.tile([P, len(PIECES)], F32, name="sums_scaled")
         total = sb.tile([P, 1], F32, name="total")
         nc.scalar.activation(sums_scaled[:], sums[:], ACT.Copy, scale=2.0 / WEIGHT_UNITS, accum_out=total[:])
         norm = sb.tile([P, 1], F32, name="norm")
         nc.vector.reciprocal(norm[:], total[:])
-        nc.vector.tensor_tensor(placed[:].indirect(listed(HALF, SLOTS)), probs[2][:], probs[2][:], ALU.add)
+        place(2)
 
         decayed = sb.tile([P, T], F32, name="decayed", tag="bias_then_decayed")
         result = sb.tile([P, T], F32, name="result")

@@ -25,6 +25,7 @@ ROW_FIRST, ROW_STEP = 11, 7
 ROW_END = ROW_FIRST + ROW_STEP * SCALE_ROWS
 FIRST = 64
 PIECES = ((0, FIRST), (FIRST, HALF), (HALF, SLOTS))
+HELD = 16
 WEIGHT_UNITS = 512.0
 HEADROOM_STEP = 32.0
 OUT_WIDTHS = (128, 128) + (256,) * 7
@@ -79,7 +80,7 @@ def tile_attend_heavyhitter_kernel(tc, query, keys_words, keys_scales, mass, dec
 
         k_words = [
             sb.tile([P, HALF], U32, name="k_words0", align_bytes=64),
-            sb.tile([P, HALF], U32, name="k_words1", tag="words_then_probs", align_bytes=64),
+            sb.tile([P, HALF], U32, name="k_words1", tag="words_then_sums", align_bytes=64),
         ]
         widths = [last - first for first, last in PIECES]
         neg_scores = [ps.tile([P, width], F32, name="neg_scores%d" % i) for i, width in enumerate(widths)]
@@ -112,10 +113,11 @@ def tile_attend_heavyhitter_kernel(tc, query, keys_words, keys_scales, mass, dec
             sb.tile([P, 1], F32, name="bias1"),
             sb.tile([P, 1], F32, name="bias2", tag="bias_then_decayed"),
         ]
-        sums = sb.tile([P, len(PIECES)], F32, name="sums")
+        early_sums = sb.tile([P, 2], F32, name="early_sums")
+        late_sums = sb.tile([P, 3], F32, name="late_sums", tag="words_then_sums", align_bytes=64)
         probs = [
             sb.tile([P, widths[0]], F32, name="probs0"),
-            sb.tile([P, widths[1]], F32, name="probs1", tag="words_then_probs", align_bytes=64),
+            sb.tile([P, widths[1]], F32, name="probs1"),
             sb.tile([P, widths[2]], F32, name="probs2"),
         ]
 
@@ -124,9 +126,9 @@ def tile_attend_heavyhitter_kernel(tc, query, keys_words, keys_scales, mass, dec
                 raised[:], neg_scores[i][:], i * HEADROOM_STEP, bias[i - 1][:], ALU.add, ALU.min, accum_out=bias[i][:]
             )
 
-        def weigh(i):
+        def weigh(i, cols, row_sum):
             nc.scalar.activation(
-                probs[i][:], neg_scores[i][:], ACT.Exp, bias=bias[i][:], scale=-1.0, accum_out=sums[:, i : i + 1]
+                probs[i][:, cols], neg_scores[i][:, cols], ACT.Exp, bias=bias[i][:], scale=-1.0, accum_out=row_sum
             )
 
         def place(i):
@@ -134,17 +136,20 @@ def tile_attend_heavyhitter_kernel(tc, query, keys_words, keys_scales, mass, dec
 
         raised1 = sb.tile([P, widths[1]], F32, name="raised1")
         nc.vector.tensor_reduce(bias[0][:], neg_scores[0][:], mybir.AxisListType.X, ALU.min)
-        weigh(0)
+        weigh(0, slice(0, widths[0]), early_sums[:, 0:1])
         chain_bias(1, raised1)
-        weigh(1)
+        weigh(1, slice(0, widths[1] - HELD), early_sums[:, 1:2])
+        weigh(1, slice(widths[1] - HELD, widths[1]), late_sums[:, 0:1])
         place(0)
         raised2 = sb.tile([P, widths[2]], F32, name="raised2", tag="bias_then_raised")
         chain_bias(2, raised2)
-        weigh(2)
+        weigh(2, slice(0, widths[2]), late_sums[:, 1:2])
         place(1)
-        sums_scaled = sb.tile([P, len(PIECES)], F32, name="sums_scaled")
+        early_copy = sb.tile([P, 2], F32, name="early_copy")
+        nc.scalar.activation(early_copy[:], early_sums[:], ACT.Copy, accum_out=late_sums[:, 2:3])
+        sums_scaled = sb.tile([P, 3], F32, name="sums_scaled")
         total = sb.tile([P, 1], F32, name="total")
-        nc.scalar.activation(sums_scaled[:], sums[:], ACT.Copy, scale=2.0 / WEIGHT_UNITS, accum_out=total[:])
+        nc.scalar.activation(sums_scaled[:], late_sums[:], ACT.Copy, scale=2.0 / WEIGHT_UNITS, accum_out=total[:])
         norm = sb.tile([P, 1], F32, name="norm")
         nc.vector.reciprocal(norm[:], total[:])
         place(2)

@@ -145,8 +145,8 @@ def tile_attend_heavyhitter_kernel(tc, query, keys_words, keys_scales, mass, dec
         chain_bias(2, raised2)
         weigh(2, slice(0, widths[2]), late_sums[:, 1:2])
         place(1)
-        early_copy = sb.tile([P, 2], F32, name="early_copy")
-        nc.scalar.activation(early_copy[:], early_sums[:], ACT.Copy, accum_out=late_sums[:, 2:3])
+        decayed = sb.tile([P, T], F32, name="decayed", tag="bias_then_decayed")
+        nc.scalar.activation(decayed[:, 0:2], early_sums[:], ACT.Copy, accum_out=late_sums[:, 2:3])
         sums_scaled = sb.tile([P, 3], F32, name="sums_scaled")
         total = sb.tile([P, 1], F32, name="total")
         nc.scalar.activation(sums_scaled[:], late_sums[:], ACT.Copy, scale=2.0 / WEIGHT_UNITS, accum_out=total[:])
@@ -154,7 +154,6 @@ def tile_attend_heavyhitter_kernel(tc, query, keys_words, keys_scales, mass, dec
         nc.vector.reciprocal(norm[:], total[:])
         place(2)
 
-        decayed = sb.tile([P, T], F32, name="decayed", tag="bias_then_decayed")
         result = sb.tile([P, T], F32, name="result")
         first = 0
         for width in OUT_WIDTHS:

@@ -68,7 +68,7 @@ def tile_attend_heavyhitter_kernel(tc, query, keys_words, keys_scales, mass, dec
 
         q_bf = sb.tile([P, Q, PACK], BF16, name="q_bf", tag="cast_then_mass", align_bytes=64)
         nc.scalar.activation(q_bf[:], q_raw[:].rearrange("p j q -> p q j"), ACT.Copy, scale=-1.0)
-        q_codes = shared.tile([P, Q], U32, name="q_codes", align_bytes=64, offset=0)
+        q_codes = shared.tile([P, Q], U32, name="q_codes", align_bytes=64, offset=T)
         q_scales = sb.tile([P, Q], U8, name="q_scales", align_bytes=64)
         nc.vector.quantize_mx(
             out=q_codes[:].bitcast(FP8X4), scales=q_scales[:], in_=q_bf[:].rearrange("p q j -> p (q j)")

@@ -57,8 +57,9 @@ def tile_attend_heavyhitter_kernel(tc, query, keys_words, keys_scales, mass, dec
         for h in range(2):
             nc.vector.memset(k_scales[h][:].bitcast(I32), 0)
 
+        spread_tags = ("spread_first", "spread_then_mass")
         for h in range(2):
-            spread_scales = sb.tile([P, HALF], U8, name="spread_scales%d" % h, align_bytes=64)
+            spread_scales = sb.tile([P, HALF], U8, name="spread_scales%d" % h, tag=spread_tags[h], align_bytes=64)
             nc.vector.tensor_copy(spread_scales[:], pool_scales[:].indirect(listed(h * HALF, (h + 1) * HALF)))
             for r in range(PACK):
                 nc.sync.dma_start(
@@ -66,7 +67,7 @@ def tile_attend_heavyhitter_kernel(tc, query, keys_words, keys_scales, mass, dec
                     spread_scales[ROW_FIRST + ROW_STEP * r : ROW_END : ROW_STEP * PACK, :].bitcast(I32),
                 )
 
-        q_bf = sb.tile([P, Q, PACK], BF16, name="q_bf", tag="cast_then_mass", align_bytes=64)
+        q_bf = sb.tile([P, Q, PACK], BF16, name="q_bf", align_bytes=64)
         nc.scalar.activation(q_bf[:], q_raw[:].rearrange("p j q -> p q j"), ACT.Copy, scale=-1.0)
         q_codes = shared.tile([P, Q], U32, name="q_codes", align_bytes=64, offset=T)
         q_scales = sb.tile([P, Q], U8, name="q_scales", align_bytes=64)
@@ -75,8 +76,9 @@ def tile_attend_heavyhitter_kernel(tc, query, keys_words, keys_scales, mass, dec
         )
         dec_sb = shared.tile([P, 1], F32, name="dec_sb", align_bytes=64, offset=T // 2)
         nc.sync.dma_start(dec_sb[:], dec)
-        mass_sb = sb.tile([P, T], F32, name="mass_sb", tag="cast_then_mass", align_bytes=64)
-        nc.sync.dma_start(mass_sb[:], mass)
+        mass_sb = sb.tile([P, T], F32, name="mass_sb", tag="spread_then_mass", align_bytes=64)
+        for cols in (slice(0, T // 2), slice(T // 2, T)):
+            nc.sync.dma_start(mass_sb[:, cols], mass[:, cols])
 
         k_words = [
             sb.tile([P, HALF], U32, name="k_words0", align_bytes=64),

@@ -23,12 +23,13 @@ HALF = SLOTS // 2
 SCALE_ROWS = D // 32
 ROW_FIRST, ROW_STEP = 11, 7
 ROW_END = ROW_FIRST + ROW_STEP * SCALE_ROWS
-FIRST = 64
-PIECES = ((0, FIRST), (FIRST, HALF), (HALF, SLOTS))
-HELD = 16
+ON_VECTOR = 128
 WEIGHT_UNITS = 512.0
-HEADROOM_STEP = 32.0
-OUT_WIDTHS = (128, 128) + (256,) * 7
+HEADROOM = 32.0
+PIECE = 256
+EARLY = 1280
+LATE = T - EARLY
+ZEROED_FIRST = 1536
 
 
 def tile_attend_heavyhitter_kernel(tc, query, keys_words, keys_scales, mass, dec, offs, out):
@@ -40,10 +41,11 @@ def tile_attend_heavyhitter_kernel(tc, query, keys_words, keys_scales, mass, dec
 
         offsets = sb.tile([P, SLOTS // GROUP], U16, name="offsets")
         q_raw = sb.tile([P, PACK, Q], F32, name="q_raw")
-        pool_scales = shared.tile([P, T], U8, name="pool_scales", align_bytes=64, offset=0)
+        pool_scales = shared.tile([P, T], U8, name="pool_scales", align_bytes=64, offset=2 * EARLY - T // 2)
         k_scales = [sb.tile([P, HALF], U8, name="k_scales%d" % h, align_bytes=64) for h in range(2)]
         pool_words = sb.tile([P, T], I32, name="pool_words", align_bytes=64)
-        placed = sb.tile([P, T], F32, name="placed")
+        placed_v = sb.tile([P, T], F32, name="placed_v")
+        placed_s = sb.tile([P, T], F32, name="placed_s")
 
         def listed(first, last):
             return offsets[:, first // GROUP : last // GROUP]
@@ -53,13 +55,13 @@ def tile_attend_heavyhitter_kernel(tc, query, keys_words, keys_scales, mass, dec
         nc.sync.dma_start(offsets[:], offs)
         nc.sync.dma_start(pool_scales[ROW_FIRST:ROW_END:ROW_STEP, :].bitcast(I32), keys_scales[0].bitcast(I32))
         nc.sync.dma_start(pool_words[:], keys_words[0].rearrange("p n t -> p (n t)").bitcast(I32))
-        nc.vector.memset(placed[:].bitcast(I32), 0)
         for h in range(2):
             nc.vector.memset(k_scales[h][:].bitcast(I32), 0)
+        nc.vector.memset(placed_v[:].bitcast(I32), 0)
+        nc.vector.memset(placed_s[:, 0:ZEROED_FIRST].bitcast(I32), 0)
 
-        spread_tags = ("spread_first", "spread_then_mass")
         for h in range(2):
-            spread_scales = sb.tile([P, HALF], U8, name="spread_scales%d" % h, tag=spread_tags[h], align_bytes=64)
+            spread_scales = sb.tile([P, HALF], U8, name="spread_scales%d" % h, align_bytes=64)
             nc.vector.tensor_copy(spread_scales[:], pool_scales[:].indirect(listed(h * HALF, (h + 1) * HALF)))
             for r in range(PACK):
                 nc.sync.dma_start(
@@ -69,100 +71,118 @@ def tile_attend_heavyhitter_kernel(tc, query, keys_words, keys_scales, mass, dec
 
         q_bf = sb.tile([P, Q, PACK], BF16, name="q_bf", align_bytes=64)
         nc.scalar.activation(q_bf[:], q_raw[:].rearrange("p j q -> p q j"), ACT.Copy, scale=-1.0)
-        q_codes = shared.tile([P, Q], U32, name="q_codes", align_bytes=64, offset=T)
+        q_codes = sb.tile([P, Q], U32, name="q_codes", align_bytes=64)
         q_scales = sb.tile([P, Q], U8, name="q_scales", align_bytes=64)
         nc.vector.quantize_mx(
             out=q_codes[:].bitcast(FP8X4), scales=q_scales[:], in_=q_bf[:].rearrange("p q j -> p (q j)")
         )
-        dec_sb = shared.tile([P, 1], F32, name="dec_sb", align_bytes=64, offset=T // 2)
+        nc.vector.memset(placed_s[:, ZEROED_FIRST:T].bitcast(I32), 0)
+        dec_sb = shared.tile([P, 1], F32, name="dec_sb", align_bytes=64, offset=2 * EARLY)
         nc.sync.dma_start(dec_sb[:], dec)
-        mass_sb = sb.tile([P, T], F32, name="mass_sb", tag="spread_then_mass", align_bytes=64)
-        for cols in (slice(0, T // 2), slice(T // 2, T)):
-            nc.sync.dma_start(mass_sb[:, cols], mass[:, cols])
+        mass_first = shared.tile([P, EARLY // 2], F32, name="mass_first", align_bytes=64, offset=0)
+        nc.sync.dma_start(mass_first[:], mass[:, 0 : EARLY // 2])
+        mass_rest = shared.tile([P, T - EARLY // 2], F32, name="mass_rest", align_bytes=64, offset=2 * EARLY + 64)
+        nc.sync.dma_start(mass_rest[:, 0 : EARLY // 2], mass[:, EARLY // 2 : EARLY])
+        nc.sync.dma_start(mass_rest[:, EARLY // 2 :], mass[:, EARLY:T])
+        mass_early = [mass_first[:], mass_rest[:, 0 : EARLY // 2]]
+        mass_late = mass_rest[:, EARLY // 2 :]
 
         k_words = [
             sb.tile([P, HALF], U32, name="k_words0", align_bytes=64),
-            sb.tile([P, HALF], U32, name="k_words1", tag="words_then_sums", align_bytes=64),
+            sb.tile([P, HALF], U32, name="k_words1", tag="words_then_sum", align_bytes=64),
         ]
-        widths = [last - first for first, last in PIECES]
-        neg_scores = [ps.tile([P, width], F32, name="neg_scores%d" % i) for i, width in enumerate(widths)]
-
-        def gather_words(h):
+        neg_scores = [ps.tile([P, HALF], F32, name="neg_scores%d" % h) for h in range(2)]
+        for h in range(2):
             nc.vector.tensor_copy(k_words[h][:], pool_words[:].bitcast(U32).indirect(listed(h * HALF, (h + 1) * HALF)))
-
-        def multiply(i, first, last):
-            h = first // HALF
-            in_half = slice(first - h * HALF, last - h * HALF)
             nc.tensor.matmul_mx(
-                out=neg_scores[i][:, first - PIECES[i][0] : last - PIECES[i][0]],
+                out=neg_scores[h][:],
                 lhsT=q_codes[:].bitcast(FP8X4),
                 lhsT_scale=q_scales[:],
-                rhs=k_words[h][:, in_half].bitcast(FP8X4),
-                rhs_scale=k_scales[h][:, in_half],
+                rhs=k_words[h][:].bitcast(FP8X4),
+                rhs_scale=k_scales[h][:],
                 start=True,
                 stop=True,
             )
 
-        gather_words(0)
-        multiply(0, 0, FIRST)
-        multiply(1, FIRST, 2 * FIRST)
-        multiply(1, 2 * FIRST, HALF)
-        gather_words(1)
-        multiply(2, HALF, SLOTS)
-
-        bias = [
-            sb.tile([P, 1], F32, name="bias0", tag="bias_then_raised"),
-            sb.tile([P, 1], F32, name="bias1"),
-            sb.tile([P, 1], F32, name="bias2", tag="bias_then_decayed"),
+        bias = [sb.tile([P, 1], F32, name="bias0", tag="bias_then_decayed"), sb.tile([P, 1], F32, name="bias1")]
+        sums = [
+            sb.tile([P, 1], F32, name="sum0", tag="words_then_sum", align_bytes=64),
+            sb.tile([P, 1], F32, name="sum1"),
         ]
-        early_sums = sb.tile([P, 2], F32, name="early_sums")
-        late_sums = sb.tile([P, 3], F32, name="late_sums", tag="words_then_sums", align_bytes=64)
-        probs = [
-            sb.tile([P, widths[0]], F32, name="probs0"),
-            sb.tile([P, widths[1]], F32, name="probs1"),
-            sb.tile([P, widths[2]], F32, name="probs2"),
-        ]
-
-        def chain_bias(i, raised):
-            nc.vector.tensor_scalar(
-                raised[:], neg_scores[i][:], i * HEADROOM_STEP, bias[i - 1][:], ALU.add, ALU.min, accum_out=bias[i][:]
-            )
-
-        def weigh(i, cols, row_sum):
-            nc.scalar.activation(
-                probs[i][:, cols], neg_scores[i][:, cols], ACT.Exp, bias=bias[i][:], scale=-1.0, accum_out=row_sum
-            )
-
-        def place(i):
-            nc.vector.tensor_tensor(placed[:].indirect(listed(*PIECES[i])), probs[i][:], probs[i][:], ALU.add)
-
-        raised1 = sb.tile([P, widths[1]], F32, name="raised1")
+        probs = sb.tile([P, SLOTS], F32, name="probs", tag="probs_then_decayed")
+        raised = sb.tile([P, HALF], F32, name="raised")
         nc.vector.tensor_reduce(bias[0][:], neg_scores[0][:], mybir.AxisListType.X, ALU.min)
-        weigh(0, slice(0, widths[0]), early_sums[:, 0:1])
-        chain_bias(1, raised1)
-        weigh(1, slice(0, widths[1] - HELD), early_sums[:, 1:2])
-        weigh(1, slice(widths[1] - HELD, widths[1]), late_sums[:, 0:1])
-        place(0)
-        raised2 = sb.tile([P, widths[2]], F32, name="raised2", tag="bias_then_raised")
-        chain_bias(2, raised2)
-        weigh(2, slice(0, widths[2]), late_sums[:, 1:2])
-        place(1)
-        decayed = sb.tile([P, T], F32, name="decayed", tag="bias_then_decayed")
-        nc.scalar.activation(decayed[:, 0:2], early_sums[:], ACT.Copy, accum_out=late_sums[:, 2:3])
-        sums_scaled = sb.tile([P, 3], F32, name="sums_scaled")
-        total = sb.tile([P, 1], F32, name="total")
-        nc.scalar.activation(sums_scaled[:], late_sums[:], ACT.Copy, scale=2.0 / WEIGHT_UNITS, accum_out=total[:])
-        norm = sb.tile([P, 1], F32, name="norm")
-        nc.vector.reciprocal(norm[:], total[:])
-        place(2)
-
-        result = sb.tile([P, T], F32, name="result")
-        first = 0
-        for width in OUT_WIDTHS:
-            cols = slice(first, first + width)
-            nc.scalar.activation(decayed[:, cols], mass_sb[:, cols], ACT.Copy, scale=dec_sb[:])
-            nc.vector.scalar_tensor_tensor(
-                result[:, cols], placed[:, cols], norm[:], decayed[:, cols], ALU.mult, ALU.add
+        nc.vector.tensor_scalar(
+            raised[:], neg_scores[1][:], HEADROOM, bias[0][:], ALU.add, ALU.min, accum_out=bias[1][:]
+        )
+        for h in range(2):
+            nc.scalar.activation(
+                probs[:, h * HALF : (h + 1) * HALF],
+                neg_scores[h][:],
+                ACT.Exp,
+                bias=bias[h][:],
+                scale=-1.0,
+                accum_out=sums[h][:],
             )
-            nc.sync.dma_start(out[:, cols], result[:, cols])
-            first = first + width
+        by_vector = probs[:, 0:ON_VECTOR]
+        nc.vector.tensor_tensor(placed_v[:].indirect(listed(0, ON_VECTOR)), by_vector, by_vector, ALU.add)
+        nc.scalar.activation(placed_s[:].indirect(listed(ON_VECTOR, SLOTS)), probs[:, ON_VECTOR:SLOTS], ACT.Copy, scale=2.0)
+
+        total = sb.tile([P, 1], F32, name="total")
+        norm = sb.tile([P, 1], F32, name="norm")
+        decayed_early = sb.tile([P, EARLY], F32, name="decayed_early", tag="bias_then_decayed")
+        decayed_late = sb.tile([P, LATE], F32, name="decayed_late", tag="probs_then_decayed")
+        partial = sb.tile([P, EARLY], F32, name="partial")
+        result = sb.tile([P, T], F32, name="result")
+
+        def decay_early(part):
+            cols = slice(part * EARLY // 2, (part + 1) * EARLY // 2)
+            nc.vector.tensor_scalar(decayed_early[:, cols], mass_early[part], dec_sb[:], None, ALU.mult)
+
+        def add_own(first, last):
+            nc.vector.scalar_tensor_tensor(
+                partial[:, first:last], placed_v[:, first:last], norm[:], decayed_early[:, first:last], ALU.mult, ALU.add
+            )
+
+        def finish_early(first, last):
+            nc.vector.scalar_tensor_tensor(
+                result[:, first:last], placed_s[:, first:last], norm[:], partial[:, first:last], ALU.mult, ALU.add
+            )
+            nc.sync.dma_start(out[:, first:last], result[:, first:last])
+
+        def join_late(first, last):
+            nc.vector.tensor_tensor(
+                joined[:, first - EARLY : last - EARLY], placed_v[:, first:last], placed_s[:, first:last], ALU.add
+            )
+
+        def finish_late(first, last):
+            nc.vector.scalar_tensor_tensor(
+                result[:, first:last],
+                joined[:, first - EARLY : last - EARLY],
+                norm[:],
+                decayed_late[:, first - EARLY : last - EARLY],
+                ALU.mult,
+                ALU.add,
+            )
+            nc.sync.dma_start(out[:, first:last], result[:, first:last])
+
+        nc.vector.tensor_scalar(total[:], sums[0][:], sums[1][:], 2.0 / WEIGHT_UNITS, ALU.add, ALU.mult)
+        decay_early(0)
+        nc.vector.reciprocal(norm[:], total[:])
+        decay_early(1)
+        add_own(0, EARLY // 2)
+        add_own(EARLY // 2, EARLY)
+        joined = sb.tile([P, LATE], F32, name="joined", tag="bias_then_decayed")
+        for first in range(0, LATE, PIECE):
+            nc.scalar.activation(
+                decayed_late[:, first : first + PIECE], mass_late[:, first : first + PIECE], ACT.Copy, scale=dec_sb[:]
+            )
+        finish_early(0, PIECE // 2)
+        finish_early(PIECE // 2, PIECE)
+        late_firsts = list(range(EARLY, T, PIECE))
+        for step, first in enumerate(range(PIECE, EARLY, PIECE)):
+            finish_early(first, first + PIECE)
+            if step < len(late_firsts):
+                join_late(late_firsts[step], late_firsts[step] + PIECE)
+        for first in late_firsts:
+            finish_late(first, first + PIECE)

@@ -1,6 +1,7 @@
 from contextlib import ExitStack
 
 import concourse.mybir as mybir
+from concourse.masks import make_identity
 
 D, T, SLOTS, Q = 512, 2048, 512, 128
 FLOPS = 2 * D * SLOTS * Q
@@ -27,7 +28,7 @@ ON_VECTOR = 128
 WEIGHT_UNITS = 512.0
 HEADROOM = 32.0
 PIECE = 256
-EARLY = 1280
+EARLY = 1408
 LATE = T - EARLY
 ZEROED_FIRST = 1536
 
@@ -50,6 +51,8 @@ def tile_attend_heavyhitter_kernel(tc, query, keys_words, keys_scales, mass, dec
         def listed(first, last):
             return offsets[:, first // GROUP : last // GROUP]
 
+        identity = sb.tile([P, P], F32, name="identity")
+        make_identity(nc, identity[:])
         nc.vector.memset(pool_scales[:].bitcast(I32), 0)
         nc.sync.dma_start(q_raw[:], query.rearrange("(p j) q -> p j q", j=PACK))
         nc.sync.dma_start(offsets[:], offs)
@@ -91,7 +94,7 @@ def tile_attend_heavyhitter_kernel(tc, query, keys_words, keys_scales, mass, dec
             sb.tile([P, HALF], U32, name="k_words0", align_bytes=64),
             sb.tile([P, HALF], U32, name="k_words1", tag="words_then_sum", align_bytes=64),
         ]
-        neg_scores = [ps.tile([P, HALF], F32, name="neg_scores%d" % h) for h in range(2)]
+        neg_scores = [ps.tile([P, HALF], F32, name="neg_scores%d" % h, tag="bank%d" % h) for h in range(2)]
         for h in range(2):
             nc.vector.tensor_copy(k_words[h][:], pool_words[:].bitcast(U32).indirect(listed(h * HALF, (h + 1) * HALF)))
             nc.tensor.matmul_mx(
@@ -150,39 +153,50 @@ def tile_attend_heavyhitter_kernel(tc, query, keys_words, keys_scales, mass, dec
             )
             nc.sync.dma_start(out[:, first:last], result[:, first:last])
 
-        def join_late(first, last):
-            nc.vector.tensor_tensor(
-                joined[:, first - EARLY : last - EARLY], placed_v[:, first:last], placed_s[:, first:last], ALU.add
-            )
-
-        def finish_late(first, last):
-            nc.vector.scalar_tensor_tensor(
-                result[:, first:last],
-                joined[:, first - EARLY : last - EARLY],
-                norm[:],
-                decayed_late[:, first - EARLY : last - EARLY],
-                ALU.mult,
-                ALU.add,
-            )
-            nc.sync.dma_start(out[:, first:last], result[:, first:last])
-
         nc.vector.tensor_scalar(total[:], sums[0][:], sums[1][:], 2.0 / WEIGHT_UNITS, ALU.add, ALU.mult)
         decay_early(0)
         nc.vector.reciprocal(norm[:], total[:])
         decay_early(1)
         add_own(0, EARLY // 2)
         add_own(EARLY // 2, EARLY)
-        joined = sb.tile([P, LATE], F32, name="joined", tag="bias_then_decayed")
-        for first in range(0, LATE, PIECE):
-            nc.scalar.activation(
-                decayed_late[:, first : first + PIECE], mass_late[:, first : first + PIECE], ACT.Copy, scale=dec_sb[:]
+        blocks = LATE // P
+        turned = [ps.tile([P, P], F32, name="turned%d" % j, tag="bank%d" % ((j + 2) % blocks)) for j in range(blocks)]
+        turned_sb = sb.tile([P, LATE], F32, name="turned_sb")
+
+        def turn(source, j, is_first):
+            nc.tensor.matmul(
+                turned[j][:],
+                source[:, EARLY + j * P : EARLY + (j + 1) * P],
+                identity[:],
+                start=is_first,
+                stop=not is_first,
+                is_transpose=True,
             )
-        finish_early(0, PIECE // 2)
-        finish_early(PIECE // 2, PIECE)
-        late_firsts = list(range(EARLY, T, PIECE))
-        for step, first in enumerate(range(PIECE, EARLY, PIECE)):
+
+        def decay_late(first, last):
+            nc.scalar.activation(decayed_late[:, first:last], mass_late[:, first:last], ACT.Copy, scale=dec_sb[:])
+
+        for j in range(blocks):
+            turn(placed_v, j, True)
+        late_pieces = [(first, min(first + PIECE, LATE)) for first in range(0, LATE, PIECE)]
+        joined = [
+            ps.tile([P, last - first], F32, name="joined%d" % i, tag="bank%d" % (blocks + i))
+            for i, (first, last) in enumerate(late_pieces)
+        ]
+        decay_late(0, 3 * P)
+        for j in range(blocks):
+            block = slice(j * P, (j + 1) * P)
+            turn(placed_s, j, False)
+            nc.scalar.copy(turned_sb[:, block], turned[j][:])
+            in_piece = j * P % PIECE
+            nc.tensor.transpose(joined[j * P // PIECE][:, in_piece : in_piece + P], turned_sb[:, block], identity[:])
+        decay_late(3 * P, LATE)
+        finish_early(0, P)
+        for first in range(P, EARLY, PIECE):
             finish_early(first, first + PIECE)
-            if step < len(late_firsts):
-                join_late(late_firsts[step], late_firsts[step] + PIECE)
-        for first in late_firsts:
-            finish_late(first, first + PIECE)
+        for i, (first, last) in enumerate(late_pieces):
+            cols = slice(EARLY + first, EARLY + last)
+            nc.vector.scalar_tensor_tensor(
+                result[:, cols], joined[i][:], norm[:], decayed_late[:, first:last], ALU.mult, ALU.add
+            )
+            nc.sync.dma_start(out[:, cols], result[:, cols])

@@ -30,7 +30,6 @@ HEADROOM = 32.0
 PIECE = 256
 EARLY = 1408
 LATE = T - EARLY
-ZEROED_FIRST = 1536
 
 
 def tile_attend_heavyhitter_kernel(tc, query, keys_words, keys_scales, mass, dec, offs, out):
@@ -38,6 +37,7 @@ def tile_attend_heavyhitter_kernel(tc, query, keys_words, keys_scales, mass, dec
     with ExitStack() as ctx:
         sb = ctx.enter_context(tc.tile_pool(name="sb", bufs=1))
         shared = ctx.enter_context(tc.tile_pool(name="shared", bufs=1))
+        after_query = ctx.enter_context(tc.tile_pool(name="after_query", bufs=1))
         ps = ctx.enter_context(tc.psum_pool(name="ps", bufs=1))
 
         offsets = sb.tile([P, SLOTS // GROUP], U16, name="offsets")
@@ -46,13 +46,10 @@ def tile_attend_heavyhitter_kernel(tc, query, keys_words, keys_scales, mass, dec
         k_scales = [sb.tile([P, HALF], U8, name="k_scales%d" % h, align_bytes=64) for h in range(2)]
         pool_words = sb.tile([P, T], I32, name="pool_words", align_bytes=64)
         placed_v = sb.tile([P, T], F32, name="placed_v")
-        placed_s = sb.tile([P, T], F32, name="placed_s")
 
         def listed(first, last):
             return offsets[:, first // GROUP : last // GROUP]
 
-        identity = sb.tile([P, P], F32, name="identity")
-        make_identity(nc, identity[:])
         nc.vector.memset(pool_scales[:].bitcast(I32), 0)
         nc.sync.dma_start(q_raw[:], query.rearrange("(p j) q -> p j q", j=PACK))
         nc.sync.dma_start(offsets[:], offs)
@@ -61,7 +58,6 @@ def tile_attend_heavyhitter_kernel(tc, query, keys_words, keys_scales, mass, dec
         for h in range(2):
             nc.vector.memset(k_scales[h][:].bitcast(I32), 0)
         nc.vector.memset(placed_v[:].bitcast(I32), 0)
-        nc.vector.memset(placed_s[:, 0:ZEROED_FIRST].bitcast(I32), 0)
 
         for h in range(2):
             spread_scales = sb.tile([P, HALF], U8, name="spread_scales%d" % h, align_bytes=64)
@@ -72,14 +68,17 @@ def tile_attend_heavyhitter_kernel(tc, query, keys_words, keys_scales, mass, dec
                     spread_scales[ROW_FIRST + ROW_STEP * r : ROW_END : ROW_STEP * PACK, :].bitcast(I32),
                 )
 
-        q_bf = sb.tile([P, Q, PACK], BF16, name="q_bf", align_bytes=64)
+        q_bf = after_query.tile([P, Q, PACK], BF16, name="q_bf", align_bytes=64, offset=0)
         nc.scalar.activation(q_bf[:], q_raw[:].rearrange("p j q -> p q j"), ACT.Copy, scale=-1.0)
         q_codes = sb.tile([P, Q], U32, name="q_codes", align_bytes=64)
         q_scales = sb.tile([P, Q], U8, name="q_scales", align_bytes=64)
         nc.vector.quantize_mx(
             out=q_codes[:].bitcast(FP8X4), scales=q_scales[:], in_=q_bf[:].rearrange("p q j -> p (q j)")
         )
-        nc.vector.memset(placed_s[:, ZEROED_FIRST:T].bitcast(I32), 0)
+        placed_s = after_query.tile([P, T], F32, name="placed_s", align_bytes=64, offset=4 * P)
+        nc.gpsimd.memset(placed_s[:].bitcast(I32), 0)
+        identity = after_query.tile([P, P], F32, name="identity", align_bytes=64, offset=0)
+        make_identity(nc, identity[:])
         dec_sb = shared.tile([P, 1], F32, name="dec_sb", align_bytes=64, offset=2 * EARLY)
         nc.sync.dma_start(dec_sb[:], dec)
         mass_first = shared.tile([P, EARLY // 2], F32, name="mass_first", align_bytes=64, offset=0)

@@ -30,6 +30,8 @@ HEADROOM = 32.0
 PIECE = 256
 EARLY = 1408
 LATE = T - EARLY
+ZEROED_FIRST = 1536
+AHEAD = 384
 
 
 def tile_attend_heavyhitter_kernel(tc, query, keys_words, keys_scales, mass, dec, offs, out):
@@ -37,19 +39,21 @@ def tile_attend_heavyhitter_kernel(tc, query, keys_words, keys_scales, mass, dec
     with ExitStack() as ctx:
         sb = ctx.enter_context(tc.tile_pool(name="sb", bufs=1))
         shared = ctx.enter_context(tc.tile_pool(name="shared", bufs=1))
-        after_query = ctx.enter_context(tc.tile_pool(name="after_query", bufs=1))
         ps = ctx.enter_context(tc.psum_pool(name="ps", bufs=1))
 
         offsets = sb.tile([P, SLOTS // GROUP], U16, name="offsets")
         q_raw = sb.tile([P, PACK, Q], F32, name="q_raw")
-        pool_scales = shared.tile([P, T], U8, name="pool_scales", align_bytes=64, offset=2 * EARLY - T // 2)
+        pool_scales = shared.tile([P, T], U8, name="pool_scales", align_bytes=64, offset=4 * EARLY - T // 2)
         k_scales = [sb.tile([P, HALF], U8, name="k_scales%d" % h, align_bytes=64) for h in range(2)]
         pool_words = sb.tile([P, T], I32, name="pool_words", align_bytes=64)
         placed_v = sb.tile([P, T], F32, name="placed_v")
+        placed_s = sb.tile([P, T], F32, name="placed_s")
 
         def listed(first, last):
             return offsets[:, first // GROUP : last // GROUP]
 
+        identity = sb.tile([P, P], F32, name="identity")
+        make_identity(nc, identity[:])
         nc.vector.memset(pool_scales[:].bitcast(I32), 0)
         nc.sync.dma_start(q_raw[:], query.rearrange("(p j) q -> p j q", j=PACK))
         nc.sync.dma_start(offsets[:], offs)
@@ -58,6 +62,7 @@ def tile_attend_heavyhitter_kernel(tc, query, keys_words, keys_scales, mass, dec
         for h in range(2):
             nc.vector.memset(k_scales[h][:].bitcast(I32), 0)
         nc.vector.memset(placed_v[:].bitcast(I32), 0)
+        nc.vector.memset(placed_s[:, 0:ZEROED_FIRST].bitcast(I32), 0)
 
         for h in range(2):
             spread_scales = sb.tile([P, HALF], U8, name="spread_scales%d" % h, align_bytes=64)
@@ -68,26 +73,20 @@ def tile_attend_heavyhitter_kernel(tc, query, keys_words, keys_scales, mass, dec
                     spread_scales[ROW_FIRST + ROW_STEP * r : ROW_END : ROW_STEP * PACK, :].bitcast(I32),
                 )
 
-        q_bf = after_query.tile([P, Q, PACK], BF16, name="q_bf", align_bytes=64, offset=0)
+        q_bf = sb.tile([P, Q, PACK], BF16, name="q_bf", align_bytes=64)
         nc.scalar.activation(q_bf[:], q_raw[:].rearrange("p j q -> p q j"), ACT.Copy, scale=-1.0)
         q_codes = sb.tile([P, Q], U32, name="q_codes", align_bytes=64)
         q_scales = sb.tile([P, Q], U8, name="q_scales", align_bytes=64)
         nc.vector.quantize_mx(
             out=q_codes[:].bitcast(FP8X4), scales=q_scales[:], in_=q_bf[:].rearrange("p q j -> p (q j)")
         )
-        placed_s = after_query.tile([P, T], F32, name="placed_s", align_bytes=64, offset=4 * P)
-        nc.gpsimd.memset(placed_s[:].bitcast(I32), 0)
-        identity = after_query.tile([P, P], F32, name="identity", align_bytes=64, offset=0)
-        make_identity(nc, identity[:])
-        dec_sb = shared.tile([P, 1], F32, name="dec_sb", align_bytes=64, offset=2 * EARLY)
+        nc.vector.memset(placed_s[:, ZEROED_FIRST:T].bitcast(I32), 0)
+        dec_sb = shared.tile([P, 1], F32, name="dec_sb", align_bytes=64, offset=4 * EARLY)
         nc.sync.dma_start(dec_sb[:], dec)
-        mass_first = shared.tile([P, EARLY // 2], F32, name="mass_first", align_bytes=64, offset=0)
-        nc.sync.dma_start(mass_first[:], mass[:, 0 : EARLY // 2])
-        mass_rest = shared.tile([P, T - EARLY // 2], F32, name="mass_rest", align_bytes=64, offset=2 * EARLY + 64)
-        nc.sync.dma_start(mass_rest[:, 0 : EARLY // 2], mass[:, EARLY // 2 : EARLY])
-        nc.sync.dma_start(mass_rest[:, EARLY // 2 :], mass[:, EARLY:T])
-        mass_early = [mass_first[:], mass_rest[:, 0 : EARLY // 2]]
-        mass_late = mass_rest[:, EARLY // 2 :]
+        mass_early = shared.tile([P, EARLY], F32, name="mass_early", align_bytes=64, offset=0)
+        nc.sync.dma_start(mass_early[:], mass[:, 0:EARLY])
+        mass_late = shared.tile([P, LATE], F32, name="mass_late", align_bytes=64, offset=4 * EARLY + 64)
+        nc.sync.dma_start(mass_late[:], mass[:, EARLY:T])
 
         k_words = [
             sb.tile([P, HALF], U32, name="k_words0", align_bytes=64),
@@ -107,10 +106,7 @@ def tile_attend_heavyhitter_kernel(tc, query, keys_words, keys_scales, mass, dec
             )
 
         bias = [sb.tile([P, 1], F32, name="bias0", tag="bias_then_decayed"), sb.tile([P, 1], F32, name="bias1")]
-        sums = [
-            sb.tile([P, 1], F32, name="sum0", tag="words_then_sum", align_bytes=64),
-            sb.tile([P, 1], F32, name="sum1"),
-        ]
+        sums = sb.tile([P, 2], F32, name="sums", tag="words_then_sum", align_bytes=64)
         probs = sb.tile([P, SLOTS], F32, name="probs", tag="probs_then_decayed")
         raised = sb.tile([P, HALF], F32, name="raised")
         nc.vector.tensor_reduce(bias[0][:], neg_scores[0][:], mybir.AxisListType.X, ALU.min)
@@ -124,22 +120,23 @@ def tile_attend_heavyhitter_kernel(tc, query, keys_words, keys_scales, mass, dec
                 ACT.Exp,
                 bias=bias[h][:],
                 scale=-1.0,
-                accum_out=sums[h][:],
+                accum_out=sums[:, h : h + 1],
             )
+        total = sb.tile([P, 1], F32, name="total")
+        sums_scaled = sb.tile([P, 2], F32, name="sums_scaled")
+        nc.scalar.activation(sums_scaled[:], sums[:], ACT.Copy, scale=2.0 / WEIGHT_UNITS, accum_out=total[:])
         by_vector = probs[:, 0:ON_VECTOR]
         nc.vector.tensor_tensor(placed_v[:].indirect(listed(0, ON_VECTOR)), by_vector, by_vector, ALU.add)
         nc.scalar.activation(placed_s[:].indirect(listed(ON_VECTOR, SLOTS)), probs[:, ON_VECTOR:SLOTS], ACT.Copy, scale=2.0)
 
-        total = sb.tile([P, 1], F32, name="total")
         norm = sb.tile([P, 1], F32, name="norm")
         decayed_early = sb.tile([P, EARLY], F32, name="decayed_early", tag="bias_then_decayed")
-        decayed_late = sb.tile([P, LATE], F32, name="decayed_late", tag="probs_then_decayed")
         partial = sb.tile([P, EARLY], F32, name="partial")
         result = sb.tile([P, T], F32, name="result")
 
         def decay_early(part):
             cols = slice(part * EARLY // 2, (part + 1) * EARLY // 2)
-            nc.vector.tensor_scalar(decayed_early[:, cols], mass_early[part], dec_sb[:], None, ALU.mult)
+            nc.vector.tensor_scalar(decayed_early[:, cols], mass_early[:, cols], dec_sb[:], None, ALU.mult)
 
         def add_own(first, last):
             nc.vector.scalar_tensor_tensor(
@@ -152,15 +149,17 @@ def tile_attend_heavyhitter_kernel(tc, query, keys_words, keys_scales, mass, dec
             )
             nc.sync.dma_start(out[:, first:last], result[:, first:last])
 
-        nc.vector.tensor_scalar(total[:], sums[0][:], sums[1][:], 2.0 / WEIGHT_UNITS, ALU.add, ALU.mult)
-        decay_early(0)
         nc.vector.reciprocal(norm[:], total[:])
+        decay_early(0)
         decay_early(1)
         add_own(0, EARLY // 2)
         add_own(EARLY // 2, EARLY)
         blocks = LATE // P
         turned = [ps.tile([P, P], F32, name="turned%d" % j, tag="bank%d" % ((j + 2) % blocks)) for j in range(blocks)]
-        turned_sb = sb.tile([P, LATE], F32, name="turned_sb")
+        turned_sb = [
+            sb.tile([P, P], F32, name="turned_sb%d" % j, tag="turned_then_decayed" if j == 0 else "turned_sb%d" % j)
+            for j in range(blocks)
+        ]
 
         def turn(source, j, is_first):
             nc.tensor.matmul(
@@ -172,30 +171,30 @@ def tile_attend_heavyhitter_kernel(tc, query, keys_words, keys_scales, mass, dec
                 is_transpose=True,
             )
 
-        def decay_late(first, last):
-            nc.scalar.activation(decayed_late[:, first:last], mass_late[:, first:last], ACT.Copy, scale=dec_sb[:])
-
         for j in range(blocks):
             turn(placed_v, j, True)
-        late_pieces = [(first, min(first + PIECE, LATE)) for first in range(0, LATE, PIECE)]
+        late_pieces = [(0, PIECE), (PIECE, AHEAD), (AHEAD, LATE)]
         joined = [
             ps.tile([P, last - first], F32, name="joined%d" % i, tag="bank%d" % (blocks + i))
             for i, (first, last) in enumerate(late_pieces)
         ]
-        decay_late(0, 3 * P)
+        decayed_ahead = sb.tile([P, AHEAD], F32, name="decayed_ahead", tag="probs_then_decayed")
+        nc.scalar.activation(decayed_ahead[:], mass_late[:, 0:AHEAD], ACT.Copy, scale=dec_sb[:])
         for j in range(blocks):
-            block = slice(j * P, (j + 1) * P)
             turn(placed_s, j, False)
-            nc.scalar.copy(turned_sb[:, block], turned[j][:])
-            in_piece = j * P % PIECE
-            nc.tensor.transpose(joined[j * P // PIECE][:, in_piece : in_piece + P], turned_sb[:, block], identity[:])
-        decay_late(3 * P, LATE)
+            nc.scalar.copy(turned_sb[j][:], turned[j][:])
+            i = [j * P < last for first, last in late_pieces].index(True)
+            in_piece = j * P - late_pieces[i][0]
+            nc.tensor.transpose(joined[i][:, in_piece : in_piece + P], turned_sb[j][:], identity[:])
+        decayed_behind = sb.tile([P, LATE - AHEAD], F32, name="decayed_behind", tag="turned_then_decayed")
+        nc.scalar.activation(decayed_behind[:], mass_late[:, AHEAD:LATE], ACT.Copy, scale=dec_sb[:])
+        decayed_late = [decayed_ahead[:, 0:PIECE], decayed_ahead[:, PIECE:AHEAD], decayed_behind[:]]
         finish_early(0, P)
         for first in range(P, EARLY, PIECE):
             finish_early(first, first + PIECE)
         for i, (first, last) in enumerate(late_pieces):
             cols = slice(EARLY + first, EARLY + last)
             nc.vector.scalar_tensor_tensor(
-                result[:, cols], joined[i][:], norm[:], decayed_late[:, first:last], ALU.mult, ALU.add
+                result[:, cols], joined[i][:], norm[:], decayed_late[i], ALU.mult, ALU.add
             )
             nc.sync.dma_start(out[:, cols], result[:, cols])

@@ -24,12 +24,14 @@ HALF = SLOTS // 2
 SCALE_ROWS = D // 32
 ROW_FIRST, ROW_STEP = 11, 7
 ROW_END = ROW_FIRST + ROW_STEP * SCALE_ROWS
-ON_VECTOR = 128
+ON_VECTOR = 160
 WEIGHT_UNITS = 512.0
 HEADROOM = 32.0
 PIECE = 256
-EARLY = 1408
+EARLY = 1280
 LATE = T - EARLY
+TURNED = 640
+JOINED = LATE - TURNED
 ZEROED_FIRST = 1536
 AHEAD = 384
 
@@ -134,27 +136,17 @@ def tile_attend_heavyhitter_kernel(tc, query, keys_words, keys_scales, mass, dec
         partial = sb.tile([P, EARLY], F32, name="partial")
         result = sb.tile([P, T], F32, name="result")
 
-        def decay_early(part):
-            cols = slice(part * EARLY // 2, (part + 1) * EARLY // 2)
-            nc.vector.tensor_scalar(decayed_early[:, cols], mass_early[:, cols], dec_sb[:], None, ALU.mult)
-
-        def add_own(first, last):
-            nc.vector.scalar_tensor_tensor(
-                partial[:, first:last], placed_v[:, first:last], norm[:], decayed_early[:, first:last], ALU.mult, ALU.add
-            )
-
-        def finish_early(first, last):
-            nc.vector.scalar_tensor_tensor(
-                result[:, first:last], placed_s[:, first:last], norm[:], partial[:, first:last], ALU.mult, ALU.add
-            )
-            nc.sync.dma_start(out[:, first:last], result[:, first:last])
+        def scale_and_add(target, weights, addend):
+            nc.vector.scalar_tensor_tensor(target, weights, norm[:], addend, ALU.mult, ALU.add)
 
         nc.vector.reciprocal(norm[:], total[:])
-        decay_early(0)
-        decay_early(1)
-        add_own(0, EARLY // 2)
-        add_own(EARLY // 2, EARLY)
-        blocks = LATE // P
+        early_halves = (slice(0, EARLY // 2), slice(EARLY // 2, EARLY))
+        for cols in early_halves:
+            nc.vector.tensor_scalar(decayed_early[:, cols], mass_early[:, cols], dec_sb[:], None, ALU.mult)
+        for cols in early_halves:
+            scale_and_add(partial[:, cols], placed_v[:, cols], decayed_early[:, cols])
+
+        blocks = TURNED // P
         turned = [ps.tile([P, P], F32, name="turned%d" % j, tag="bank%d" % ((j + 2) % blocks)) for j in range(blocks)]
         turned_sb = [
             sb.tile([P, P], F32, name="turned_sb%d" % j, tag="turned_then_decayed" if j == 0 else "turned_sb%d" % j)
@@ -162,9 +154,10 @@ def tile_attend_heavyhitter_kernel(tc, query, keys_words, keys_scales, mass, dec
         ]
 
         def turn(source, j, is_first):
+            first = T - TURNED + j * P
             nc.tensor.matmul(
                 turned[j][:],
-                source[:, EARLY + j * P : EARLY + (j + 1) * P],
+                source[:, first : first + P],
                 identity[:],
                 start=is_first,
                 stop=not is_first,
@@ -173,28 +166,37 @@ def tile_attend_heavyhitter_kernel(tc, query, keys_words, keys_scales, mass, dec
 
         for j in range(blocks):
             turn(placed_v, j, True)
-        late_pieces = [(0, PIECE), (PIECE, AHEAD), (AHEAD, LATE)]
-        joined = [
-            ps.tile([P, last - first], F32, name="joined%d" % i, tag="bank%d" % (blocks + i))
-            for i, (first, last) in enumerate(late_pieces)
+        turned_pieces = [(first, min(first + PIECE, T)) for first in range(T - TURNED, T, PIECE)]
+        summed = [
+            ps.tile([P, last - first], F32, name="summed%d" % i, tag="bank%d" % (blocks + i))
+            for i, (first, last) in enumerate(turned_pieces)
         ]
         decayed_ahead = sb.tile([P, AHEAD], F32, name="decayed_ahead", tag="probs_then_decayed")
         nc.scalar.activation(decayed_ahead[:], mass_late[:, 0:AHEAD], ACT.Copy, scale=dec_sb[:])
         for j in range(blocks):
             turn(placed_s, j, False)
             nc.scalar.copy(turned_sb[j][:], turned[j][:])
-            i = [j * P < last for first, last in late_pieces].index(True)
-            in_piece = j * P - late_pieces[i][0]
-            nc.tensor.transpose(joined[i][:, in_piece : in_piece + P], turned_sb[j][:], identity[:])
+            in_piece = j * P % PIECE
+            nc.tensor.transpose(summed[j * P // PIECE][:, in_piece : in_piece + P], turned_sb[j][:], identity[:])
         decayed_behind = sb.tile([P, LATE - AHEAD], F32, name="decayed_behind", tag="turned_then_decayed")
         nc.scalar.activation(decayed_behind[:], mass_late[:, AHEAD:LATE], ACT.Copy, scale=dec_sb[:])
-        decayed_late = [decayed_ahead[:, 0:PIECE], decayed_ahead[:, PIECE:AHEAD], decayed_behind[:]]
-        finish_early(0, P)
-        for first in range(P, EARLY, PIECE):
-            finish_early(first, first + PIECE)
-        for i, (first, last) in enumerate(late_pieces):
-            cols = slice(EARLY + first, EARLY + last)
-            nc.vector.scalar_tensor_tensor(
-                result[:, cols], joined[i][:], norm[:], decayed_late[i], ALU.mult, ALU.add
-            )
-            nc.sync.dma_start(out[:, cols], result[:, cols])
+
+        def decayed_late(first, last):
+            if last - EARLY <= AHEAD:
+                return decayed_ahead[:, first - EARLY : last - EARLY]
+            return decayed_behind[:, first - EARLY - AHEAD : last - EARLY - AHEAD]
+
+        joined = sb.tile([P, JOINED], F32, name="joined", tag="bias_then_decayed")
+        between = slice(EARLY, EARLY + JOINED)
+        edges = [0] + list(range(P, EARLY + JOINED + 1, PIECE))
+        for first, last in zip(edges[:-1], edges[1:]):
+            own = slice(first, min(last, EARLY))
+            scale_and_add(result[:, own], placed_s[:, own], partial[:, own])
+            if last == edges[-3]:
+                nc.vector.tensor_tensor(joined[:], placed_v[:, between], placed_s[:, between], ALU.add)
+            if last > EARLY:
+                scale_and_add(result[:, between], joined[:], decayed_late(EARLY, EARLY + JOINED))
+            nc.sync.dma_start(out[:, first:last], result[:, first:last])
+        for i, (first, last) in enumerate(turned_pieces):
+            scale_and_add(result[:, first:last], summed[i][:], decayed_late(first, last))
+            nc.sync.dma_start(out[:, first:last], result[:, first:last])

@@ -32,7 +32,6 @@ EARLY = 1280
 LATE = T - EARLY
 TURNED = 640
 JOINED = LATE - TURNED
-ZEROED_FIRST = 1536
 AHEAD = 384
 
 
@@ -41,6 +40,7 @@ def tile_attend_heavyhitter_kernel(tc, query, keys_words, keys_scales, mass, dec
     with ExitStack() as ctx:
         sb = ctx.enter_context(tc.tile_pool(name="sb", bufs=1))
         shared = ctx.enter_context(tc.tile_pool(name="shared", bufs=1))
+        after_query = ctx.enter_context(tc.tile_pool(name="after_query", bufs=1))
         ps = ctx.enter_context(tc.psum_pool(name="ps", bufs=1))
 
         offsets = sb.tile([P, SLOTS // GROUP], U16, name="offsets")
@@ -49,13 +49,10 @@ def tile_attend_heavyhitter_kernel(tc, query, keys_words, keys_scales, mass, dec
         k_scales = [sb.tile([P, HALF], U8, name="k_scales%d" % h, align_bytes=64) for h in range(2)]
         pool_words = sb.tile([P, T], I32, name="pool_words", align_bytes=64)
         placed_v = sb.tile([P, T], F32, name="placed_v")
-        placed_s = sb.tile([P, T], F32, name="placed_s")
 
         def listed(first, last):
             return offsets[:, first // GROUP : last // GROUP]
 
-        identity = sb.tile([P, P], F32, name="identity")
-        make_identity(nc, identity[:])
         nc.vector.memset(pool_scales[:].bitcast(I32), 0)
         nc.sync.dma_start(q_raw[:], query.rearrange("(p j) q -> p j q", j=PACK))
         nc.sync.dma_start(offsets[:], offs)
@@ -64,7 +61,6 @@ def tile_attend_heavyhitter_kernel(tc, query, keys_words, keys_scales, mass, dec
         for h in range(2):
             nc.vector.memset(k_scales[h][:].bitcast(I32), 0)
         nc.vector.memset(placed_v[:].bitcast(I32), 0)
-        nc.vector.memset(placed_s[:, 0:ZEROED_FIRST].bitcast(I32), 0)
 
         for h in range(2):
             spread_scales = sb.tile([P, HALF], U8, name="spread_scales%d" % h, align_bytes=64)
@@ -75,14 +71,17 @@ def tile_attend_heavyhitter_kernel(tc, query, keys_words, keys_scales, mass, dec
                     spread_scales[ROW_FIRST + ROW_STEP * r : ROW_END : ROW_STEP * PACK, :].bitcast(I32),
                 )
 
-        q_bf = sb.tile([P, Q, PACK], BF16, name="q_bf", align_bytes=64)
+        q_bf = after_query.tile([P, Q, PACK], BF16, name="q_bf", align_bytes=64, offset=0)
         nc.scalar.activation(q_bf[:], q_raw[:].rearrange("p j q -> p q j"), ACT.Copy, scale=-1.0)
         q_codes = sb.tile([P, Q], U32, name="q_codes", align_bytes=64)
         q_scales = sb.tile([P, Q], U8, name="q_scales", align_bytes=64)
         nc.vector.quantize_mx(
             out=q_codes[:].bitcast(FP8X4), scales=q_scales[:], in_=q_bf[:].rearrange("p q j -> p (q j)")
         )
-        nc.vector.memset(placed_s[:, ZEROED_FIRST:T].bitcast(I32), 0)
+        identity = after_query.tile([P, P], F32, name="identity", align_bytes=64, offset=0)
+        make_identity(nc, identity[:])
+        placed_s = after_query.tile([P, T], F32, name="placed_s", align_bytes=64, offset=4 * P)
+        nc.gpsimd.memset(placed_s[:].bitcast(I32), 0)
         dec_sb = shared.tile([P, 1], F32, name="dec_sb", align_bytes=64, offset=4 * EARLY)
         nc.sync.dma_start(dec_sb[:], dec)
         mass_early = shared.tile([P, EARLY], F32, name="mass_early", align_bytes=64, offset=0)

@@ -30,6 +30,7 @@ HEADROOM = 32.0
 PIECE = 256
 EARLY = 1280
 LATE = T - EARLY
+ZEROED_FIRST = 1536
 TURNED = 640
 JOINED = LATE - TURNED
 AHEAD = 384
@@ -40,7 +41,6 @@ def tile_attend_heavyhitter_kernel(tc, query, keys_words, keys_scales, mass, dec
     with ExitStack() as ctx:
         sb = ctx.enter_context(tc.tile_pool(name="sb", bufs=1))
         shared = ctx.enter_context(tc.tile_pool(name="shared", bufs=1))
-        after_query = ctx.enter_context(tc.tile_pool(name="after_query", bufs=1))
         ps = ctx.enter_context(tc.psum_pool(name="ps", bufs=1))
 
         offsets = sb.tile([P, SLOTS // GROUP], U16, name="offsets")
@@ -49,10 +49,13 @@ def tile_attend_heavyhitter_kernel(tc, query, keys_words, keys_scales, mass, dec
         k_scales = [sb.tile([P, HALF], U8, name="k_scales%d" % h, align_bytes=64) for h in range(2)]
         pool_words = sb.tile([P, T], I32, name="pool_words", align_bytes=64)
         placed_v = sb.tile([P, T], F32, name="placed_v")
+        placed_s = sb.tile([P, T], F32, name="placed_s")
 
         def listed(first, last):
             return offsets[:, first // GROUP : last // GROUP]
 
+        identity = sb.tile([P, P], F32, name="identity")
+        make_identity(nc, identity[:])
         nc.vector.memset(pool_scales[:].bitcast(I32), 0)
         nc.sync.dma_start(q_raw[:], query.rearrange("(p j) q -> p j q", j=PACK))
         nc.sync.dma_start(offsets[:], offs)
@@ -61,6 +64,7 @@ def tile_attend_heavyhitter_kernel(tc, query, keys_words, keys_scales, mass, dec
         for h in range(2):
             nc.vector.memset(k_scales[h][:].bitcast(I32), 0)
         nc.vector.memset(placed_v[:].bitcast(I32), 0)
+        nc.vector.memset(placed_s[:, 0:ZEROED_FIRST].bitcast(I32), 0)
 
         for h in range(2):
             spread_scales = sb.tile([P, HALF], U8, name="spread_scales%d" % h, align_bytes=64)
@@ -71,17 +75,14 @@ def tile_attend_heavyhitter_kernel(tc, query, keys_words, keys_scales, mass, dec
                     spread_scales[ROW_FIRST + ROW_STEP * r : ROW_END : ROW_STEP * PACK, :].bitcast(I32),
                 )
 
-        q_bf = after_query.tile([P, Q, PACK], BF16, name="q_bf", align_bytes=64, offset=0)
+        q_bf = sb.tile([P, Q, PACK], BF16, name="q_bf", align_bytes=64)
         nc.scalar.activation(q_bf[:], q_raw[:].rearrange("p j q -> p q j"), ACT.Copy, scale=-1.0)
         q_codes = sb.tile([P, Q], U32, name="q_codes", align_bytes=64)
         q_scales = sb.tile([P, Q], U8, name="q_scales", align_bytes=64)
         nc.vector.quantize_mx(
             out=q_codes[:].bitcast(FP8X4), scales=q_scales[:], in_=q_bf[:].rearrange("p q j -> p (q j)")
         )
-        identity = after_query.tile([P, P], F32, name="identity", align_bytes=64, offset=0)
-        make_identity(nc, identity[:])
-        placed_s = after_query.tile([P, T], F32, name="placed_s", align_bytes=64, offset=4 * P)
-        nc.gpsimd.memset(placed_s[:].bitcast(I32), 0)
+        nc.vector.memset(placed_s[:, ZEROED_FIRST:T].bitcast(I32), 0)
         dec_sb = shared.tile([P, 1], F32, name="dec_sb", align_bytes=64, offset=4 * EARLY)
         nc.sync.dma_start(dec_sb[:], dec)
         mass_early = shared.tile([P, EARLY], F32, name="mass_early", align_bytes=64, offset=0)
@@ -178,7 +179,13 @@ def tile_attend_heavyhitter_kernel(tc, query, keys_words, keys_scales, mass, dec
             in_piece = j * P % PIECE
             nc.tensor.transpose(summed[j * P // PIECE][:, in_piece : in_piece + P], turned_sb[j][:], identity[:])
         decayed_behind = sb.tile([P, LATE - AHEAD], F32, name="decayed_behind", tag="turned_then_decayed")
-        nc.scalar.activation(decayed_behind[:], mass_late[:, AHEAD:LATE], ACT.Copy, scale=dec_sb[:])
+        for first, last in turned_pieces[1:]:
+            nc.scalar.activation(
+                decayed_behind[:, first - EARLY - AHEAD : last - EARLY - AHEAD],
+                mass_late[:, first - EARLY : last - EARLY],
+                ACT.Copy,
+                scale=dec_sb[:],
+            )
 
         def decayed_late(first, last):
             if last - EARLY <= AHEAD:

@@ -24,16 +24,15 @@ HALF = SLOTS // 2
 SCALE_ROWS = D // 32
 ROW_FIRST, ROW_STEP = 11, 7
 ROW_END = ROW_FIRST + ROW_STEP * SCALE_ROWS
-ON_VECTOR = 160
+ON_VECTOR = 128
 WEIGHT_UNITS = 512.0
 HEADROOM = 32.0
 PIECE = 256
-EARLY = 1280
+EARLY = 1408
 LATE = T - EARLY
 ZEROED_FIRST = 1536
 TURNED = 640
-JOINED = LATE - TURNED
-AHEAD = 384
+AHEAD = 256
 
 
 def tile_attend_heavyhitter_kernel(tc, query, keys_words, keys_scales, mass, dec, offs, out):
@@ -192,16 +191,9 @@ def tile_attend_heavyhitter_kernel(tc, query, keys_words, keys_scales, mass, dec
                 return decayed_ahead[:, first - EARLY : last - EARLY]
             return decayed_behind[:, first - EARLY - AHEAD : last - EARLY - AHEAD]
 
-        joined = sb.tile([P, JOINED], F32, name="joined", tag="bias_then_decayed")
-        between = slice(EARLY, EARLY + JOINED)
-        edges = [0] + list(range(P, EARLY + JOINED + 1, PIECE))
+        edges = [0] + list(range(P, EARLY + 1, PIECE))
         for first, last in zip(edges[:-1], edges[1:]):
-            own = slice(first, min(last, EARLY))
-            scale_and_add(result[:, own], placed_s[:, own], partial[:, own])
-            if last == edges[-3]:
-                nc.vector.tensor_tensor(joined[:], placed_v[:, between], placed_s[:, between], ALU.add)
-            if last > EARLY:
-                scale_and_add(result[:, between], joined[:], decayed_late(EARLY, EARLY + JOINED))
+            scale_and_add(result[:, first:last], placed_s[:, first:last], partial[:, first:last])
             nc.sync.dma_start(out[:, first:last], result[:, first:last])
         for i, (first, last) in enumerate(turned_pieces):
             scale_and_add(result[:, first:last], summed[i][:], decayed_late(first, last))

from contextlib import ExitStack

import concourse.mybir as mybir
from concourse.masks import make_identity

D, T, SLOTS, Q = 512, 2048, 512, 128
FLOPS = 2 * D * SLOTS * Q

F32 = mybir.dt.float32
BF16 = mybir.dt.bfloat16
I32 = mybir.dt.int32
U32 = mybir.dt.uint32
U16 = mybir.dt.uint16
U8 = mybir.dt.uint8
FP8X4 = mybir.dt.float8_e4m3fn_x4
ALU = mybir.AluOpType
ACT = mybir.ActivationFunctionType

P = 128
QUADRANT = 32
PACK = 4
GROUP = 16
HALF = SLOTS // 2
SCALE_ROWS = D // 32
ROW_FIRST, ROW_STEP = 11, 7
ROW_END = ROW_FIRST + ROW_STEP * SCALE_ROWS
ON_VECTOR = 128
WEIGHT_UNITS = 512.0
HEADROOM = 32.0
PIECE = 256
EARLY = 1408
LATE = T - EARLY
ZEROED_FIRST = 1536
TURNED = 640
AHEAD = 256


def tile_attend_heavyhitter_kernel(tc, query, keys_words, keys_scales, mass, dec, offs, out):
    nc = tc.nc
    with ExitStack() as ctx:
        sb = ctx.enter_context(tc.tile_pool(name="sb", bufs=1))
        shared = ctx.enter_context(tc.tile_pool(name="shared", bufs=1))
        ps = ctx.enter_context(tc.psum_pool(name="ps", bufs=1))

        offsets = sb.tile([P, SLOTS // GROUP], U16, name="offsets")
        q_raw = sb.tile([P, PACK, Q], F32, name="q_raw")
        pool_scales = shared.tile([P, T], U8, name="pool_scales", align_bytes=64, offset=4 * EARLY - T // 2)
        k_scales = [sb.tile([P, HALF], U8, name="k_scales%d" % h, align_bytes=64) for h in range(2)]
        pool_words = sb.tile([P, T], I32, name="pool_words", align_bytes=64)
        placed_v = sb.tile([P, T], F32, name="placed_v")
        placed_s = sb.tile([P, T], F32, name="placed_s")

        def listed(first, last):
            return offsets[:, first // GROUP : last // GROUP]

        identity = sb.tile([P, P], F32, name="identity")
        make_identity(nc, identity[:])
        nc.vector.memset(pool_scales[:].bitcast(I32), 0)
        nc.sync.dma_start(q_raw[:], query.rearrange("(p j) q -> p j q", j=PACK))
        nc.sync.dma_start(offsets[:], offs)
        nc.sync.dma_start(pool_scales[ROW_FIRST:ROW_END:ROW_STEP, :].bitcast(I32), keys_scales[0].bitcast(I32))
        nc.sync.dma_start(pool_words[:], keys_words[0].rearrange("p n t -> p (n t)").bitcast(I32))
        for h in range(2):
            nc.vector.memset(k_scales[h][:].bitcast(I32), 0)
        nc.vector.memset(placed_v[:].bitcast(I32), 0)
        nc.vector.memset(placed_s[:, 0:ZEROED_FIRST].bitcast(I32), 0)

        for h in range(2):
            spread_scales = sb.tile([P, HALF], U8, name="spread_scales%d" % h, align_bytes=64)
            nc.vector.tensor_copy(spread_scales[:], pool_scales[:].indirect(listed(h * HALF, (h + 1) * HALF)))
            for r in range(PACK):
                nc.sync.dma_start(
                    k_scales[h][r:P:QUADRANT, :].bitcast(I32),
                    spread_scales[ROW_FIRST + ROW_STEP * r : ROW_END : ROW_STEP * PACK, :].bitcast(I32),
                )

        q_bf = sb.tile([P, Q, PACK], BF16, name="q_bf", align_bytes=64)
        nc.scalar.activation(q_bf[:], q_raw[:].rearrange("p j q -> p q j"), ACT.Copy, scale=-1.0)
        q_codes = sb.tile([P, Q], U32, name="q_codes", align_bytes=64)
        q_scales = sb.tile([P, Q], U8, name="q_scales", align_bytes=64)
        nc.vector.quantize_mx(
            out=q_codes[:].bitcast(FP8X4), scales=q_scales[:], in_=q_bf[:].rearrange("p q j -> p (q j)")
        )
        nc.vector.memset(placed_s[:, ZEROED_FIRST:T].bitcast(I32), 0)
        dec_sb = shared.tile([P, 1], F32, name="dec_sb", align_bytes=64, offset=4 * EARLY)
        nc.sync.dma_start(dec_sb[:], dec)
        mass_early = shared.tile([P, EARLY], F32, name="mass_early", align_bytes=64, offset=0)
        nc.sync.dma_start(mass_early[:], mass[:, 0:EARLY])
        mass_late = shared.tile([P, LATE], F32, name="mass_late", align_bytes=64, offset=4 * EARLY + 64)
        nc.sync.dma_start(mass_late[:], mass[:, EARLY:T])

        k_words = [
            sb.tile([P, HALF], U32, name="k_words0", align_bytes=64),
            sb.tile([P, HALF], U32, name="k_words1", tag="words_then_sum", align_bytes=64),
        ]
        neg_scores = [ps.tile([P, HALF], F32, name="neg_scores%d" % h, tag="bank%d" % h) for h in range(2)]
        for h in range(2):
            nc.vector.tensor_copy(k_words[h][:], pool_words[:].bitcast(U32).indirect(listed(h * HALF, (h + 1) * HALF)))
            nc.tensor.matmul_mx(
                out=neg_scores[h][:],
                lhsT=q_codes[:].bitcast(FP8X4),
                lhsT_scale=q_scales[:],
                rhs=k_words[h][:].bitcast(FP8X4),
                rhs_scale=k_scales[h][:],
                start=True,
                stop=True,
            )

        bias = [sb.tile([P, 1], F32, name="bias0", tag="bias_then_decayed"), sb.tile([P, 1], F32, name="bias1")]
        sums = sb.tile([P, 2], F32, name="sums", tag="words_then_sum", align_bytes=64)
        probs = sb.tile([P, SLOTS], F32, name="probs", tag="probs_then_decayed")
        raised = sb.tile([P, HALF], F32, name="raised")
        nc.vector.tensor_reduce(bias[0][:], neg_scores[0][:], mybir.AxisListType.X, ALU.min)
        nc.vector.tensor_scalar(
            raised[:], neg_scores[1][:], HEADROOM, bias[0][:], ALU.add, ALU.min, accum_out=bias[1][:]
        )
        for h in range(2):
            nc.scalar.activation(
                probs[:, h * HALF : (h + 1) * HALF],
                neg_scores[h][:],
                ACT.Exp,
                bias=bias[h][:],
                scale=-1.0,
                accum_out=sums[:, h : h + 1],
            )
        total = sb.tile([P, 1], F32, name="total")
        sums_scaled = sb.tile([P, 2], F32, name="sums_scaled")
        nc.scalar.activation(sums_scaled[:], sums[:], ACT.Copy, scale=2.0 / WEIGHT_UNITS, accum_out=total[:])
        by_vector = probs[:, 0:ON_VECTOR]
        nc.vector.tensor_tensor(placed_v[:].indirect(listed(0, ON_VECTOR)), by_vector, by_vector, ALU.add)
        nc.scalar.activation(placed_s[:].indirect(listed(ON_VECTOR, SLOTS)), probs[:, ON_VECTOR:SLOTS], ACT.Copy, scale=2.0)

        norm = sb.tile([P, 1], F32, name="norm")
        decayed_early = sb.tile([P, EARLY], F32, name="decayed_early", tag="bias_then_decayed")
        partial = sb.tile([P, EARLY], F32, name="partial")
        result = sb.tile([P, T], F32, name="result")

        def scale_and_add(target, weights, addend):
            nc.vector.scalar_tensor_tensor(target, weights, norm[:], addend, ALU.mult, ALU.add)

        nc.vector.reciprocal(norm[:], total[:])
        early_halves = (slice(0, EARLY // 2), slice(EARLY // 2, EARLY))
        for cols in early_halves:
            nc.vector.tensor_scalar(decayed_early[:, cols], mass_early[:, cols], dec_sb[:], None, ALU.mult)
        for cols in early_halves:
            scale_and_add(partial[:, cols], placed_v[:, cols], decayed_early[:, cols])

        blocks = TURNED // P
        turned = [ps.tile([P, P], F32, name="turned%d" % j, tag="bank%d" % ((j + 2) % blocks)) for j in range(blocks)]
        turned_sb = [
            sb.tile([P, P], F32, name="turned_sb%d" % j, tag="turned_then_decayed" if j == 0 else "turned_sb%d" % j)
            for j in range(blocks)
        ]

        def turn(source, j, is_first):
            first = T - TURNED + j * P
            nc.tensor.matmul(
                turned[j][:],
                source[:, first : first + P],
                identity[:],
                start=is_first,
                stop=not is_first,
                is_transpose=True,
            )

        for j in range(blocks):
            turn(placed_v, j, True)
        turned_pieces = [(first, min(first + PIECE, T)) for first in range(T - TURNED, T, PIECE)]
        summed = [
            ps.tile([P, last - first], F32, name="summed%d" % i, tag="bank%d" % (blocks + i))
            for i, (first, last) in enumerate(turned_pieces)
        ]
        decayed_ahead = sb.tile([P, AHEAD], F32, name="decayed_ahead", tag="probs_then_decayed")
        nc.scalar.activation(decayed_ahead[:], mass_late[:, 0:AHEAD], ACT.Copy, scale=dec_sb[:])
        for j in range(blocks):
            turn(placed_s, j, False)
            nc.scalar.copy(turned_sb[j][:], turned[j][:])
            in_piece = j * P % PIECE
            nc.tensor.transpose(summed[j * P // PIECE][:, in_piece : in_piece + P], turned_sb[j][:], identity[:])
        decayed_behind = sb.tile([P, LATE - AHEAD], F32, name="decayed_behind", tag="turned_then_decayed")
        for first, last in turned_pieces[1:]:
            nc.scalar.activation(
                decayed_behind[:, first - EARLY - AHEAD : last - EARLY - AHEAD],
                mass_late[:, first - EARLY : last - EARLY],
                ACT.Copy,
                scale=dec_sb[:],
            )

        def decayed_late(first, last):
            if last - EARLY <= AHEAD:
                return decayed_ahead[:, first - EARLY : last - EARLY]
            return decayed_behind[:, first - EARLY - AHEAD : last - EARLY - AHEAD]

        edges = [0] + list(range(P, EARLY + 1, PIECE))
        for first, last in zip(edges[:-1], edges[1:]):
            scale_and_add(result[:, first:last], placed_s[:, first:last], partial[:, first:last])
            nc.sync.dma_start(out[:, first:last], result[:, first:last])
        for i, (first, last) in enumerate(turned_pieces):
            scale_and_add(result[:, first:last], summed[i][:], decayed_late(first, last))
            nc.sync.dma_start(out[:, first:last], result[:, first:last])
